import numpy as np, ml_dtypes
CORES = [3,11,19,27,35,43,51,59]
N = 8
import mx_ref
BF = ml_dtypes.bfloat16
def gcols(t, e):
    v = np.concatenate([t.reshape(8, 16, -1, 4), np.zeros((8, 16, 1, 4), BF)], axis=2)
    return np.ascontiguousarray(np.stack([v[g][:, e[g]] for g in range(8)])).reshape(128, -1)
def tile(rs):
    return np.stack(rs, axis=2).reshape(128, -1).astype(BF)
def pick(q, e):
    c = np.concatenate([q[0].reshape(128, -1, 4), np.zeros((128, 1, 4), np.uint8)], axis=1); s = np.concatenate([q[1], np.ones((16, 1), np.uint8)], axis=1)
    return (np.ascontiguousarray(c[:, e].reshape(128, -1)), np.ascontiguousarray(s[:, e]))
def join(*qs):
    return (np.concatenate([q[0] for q in qs], axis=1), np.concatenate([q[1] for q in qs], axis=1))
def put(q, e, v):
    c, s = q[0].reshape(128, -1, 4).copy(), q[1].copy(); c[:, e] = v[0].reshape(128, -1, 4); s[:, e] = v[1]
    return (c.reshape(128, -1), s)
def pk(c, s):
    return (np.ascontiguousarray(c), mx_ref.live(s))
def emit(q):
    return q[0], q[1]
def packed(v, rng):
    q = [mx_ref.quantize(np.ascontiguousarray(v[r])) for r in range(N)]
    return np.stack([a for a, b in q]), np.stack([mx_ref.plane(b, rng) for a, b in q])
def values_of_codes():
    e, c = np.zeros((128, 128, 4), np.float32), np.zeros((128, 2, 4), np.uint8)
    e[np.arange(128), np.arange(128), 0] = 1
    c[:127, :, 0] = np.arange(256).reshape(2, 128).T[:127]
    return mx_ref.matmul(mx_ref.quantize(e.reshape(128, 512).astype(BF)), (c.reshape(128, 8), np.full((16, 2), 127, np.uint8))).T.reshape(-1).astype(np.float64)
CODE_VALUE, SCALE_VALUE = values_of_codes(), 2.0 ** (np.arange(256) - 127.0)
def decode(q):
    return (CODE_VALUE[q[0]].reshape(16, 8, -1, 4) * SCALE_VALUE[q[1]][:, None, :, None] + 0.0).reshape(128, -1).astype(np.float32)
def f(rng, *shape):
    return mx_ref.flush((rng.standard_normal(shape, dtype=np.float32) * np.exp2(rng.integers(-2, 3, shape[:-1] + (1,)))).astype(BF))
def wide(rng, *shape, cols=0):
    v = rng.standard_normal(shape, dtype=np.float32) * np.exp2(rng.integers(-12, 13, shape)).astype(np.float32)
    if cols: v *= np.repeat(np.exp2(rng.integers(-cols, cols + 1, shape[:-2] + (1, shape[-1] // 4))) * (rng.random(shape[:-2] + (1, shape[-1] // 4)) > 0.0625), 4, axis=-1).astype(np.float32)
    return mx_ref.flush(v.astype(BF))
C, STEP = 256, [1, 2, 4]
def numbers_of(rng):
    return {"x": np.array(f(rng, N, 128, 4 * C)), "u": np.array(f(rng, N, 128, 512)), "v": np.array(f(rng, N, 128, 512))}
def layers(rng):
    return np.array(f(rng, N, 128, 2048)).reshape(N, 8, 16, 4, 8, 16, 4)
def weights(rng, w):
    c, p = packed(np.ascontiguousarray(w).reshape(N, 128, 2048), rng)
    return {"wc": c, "ws": p}
def both(x, u):
    return {"x": x.astype(np.float32).reshape(N, 128, 4 * C).astype(BF), "u": u.astype(np.float32).reshape(N, 128, 512).astype(BF)}
def setup_inputs(rng):
    return {**numbers_of(rng), **weights(rng, layers(rng))}
def setup_inputs_ties(rng):
    d = numbers_of(rng)
    e = rng.permutation(N)
    x = rng.integers(-1, 2, (N, 128, C, 4)) * (rng.random((N, 128, C, 4)) < 0.09375)
    u = rng.integers(-1, 2, (N, 128, 128, 4)) * (rng.random((N, 128, 128, 4)) < 0.09375)
    x[e[0]] = x[e[0]][:, :1].copy()
    x[e[1]] = 0
    u[e[2]] = u[e[2]][:, :1].copy()
    w = np.zeros((N, 128, 512, 4), np.float32)
    for r in range(N):
        a, c = rng.permutation(512)[:128], rng.permutation(512)[:128]
        w[r, a // 4, c, a % 4] = 64
    return {**both(x, u), "v": d["v"], **weights(rng, w.astype(BF))}
def setup_inputs_near(rng):
    d = numbers_of(rng)
    h, o = rng.permutation(8), rng.permutation(N) % 4
    x = d["x"].astype(np.float32).reshape(N, 8, 16, C, 4)
    u = d["u"].astype(np.float32).reshape(N, 8, 16, 128, 4)
    x[:, :, 8:] = 0
    u[:, :, :8] = 0
    x[:, h[:2], :8] = 0
    p = np.exp2(np.arange(4) - 23.0)
    for r in range(N):
        k = 1.0 if o[r] < 2 else 2.0 ** -29
        if o[r] == 3:
            x[r, h[0], 0, :, 0] = rng.choice([1.0, 1.125], C) * 2.0 ** -30
            u[r, h[0], 0, :, 0] = rng.choice([1.125, 1.25], 128) * 2.0 ** -30
        else:
            x[r, h[0], 0, :, 0] = -1.0 if o[r] == 1 else 1.0
            u[r, h[0], 0, :, 0] = k
            x[r, h[1], 0] = ((rng.integers(0, 16, (C, 1)) >> np.arange(4)) & 1) * p
            u[r, h[1], 0] = k
            x[r, h[1], 1] = p
            u[r, h[1], 1] = ((rng.integers(0, 16, (128, 1)) >> np.arange(4)) & 1) * k
            x[r, h[1], 2, :, 0] = 2.0 ** -10
            u[r, h[1], 2, :, 0] = k
        x[r, h[0], 0, rng.integers(C), 0] = 2.0 ** 29
    w = layers(rng)
    w[:, h[:2], :8] = 0
    for g in h[:2]: w[:, :, :, :, g, :8] = 0
    return {**both(x, u), "v": d["v"], **weights(rng, w)}
def setup_inputs_huge(rng):
    d = numbers_of(rng)
    e = rng.permutation(N)
    x = 0.7 + 0.3 * rng.random((N, 8, 16, C, 4))
    u = 0.7 + 0.3 * rng.random((N, 8, 16, 128, 4))
    for i in range(N):
        r = e[i]
        if i == 0:
            x[r] = -0.94 - 0.06 * rng.random((8, 16, C, 4))
            x[r][:, :, rng.permutation(C)[:4]] *= -1.0
            u[r] = 0.94 + 0.06 * rng.random((8, 16, 128, 4))
        elif i % 2 == 1: u[r] *= -1.0
        else:
            x[r] *= rng.choice([-1.0, 1.0], (1, 1, C, 1))
            u[r] *= rng.choice([-1.0, 1.0], (1, 1, 128, 1))
    w = np.zeros((N, 128, 4, 128, 4), np.float32)
    i = np.arange(128)
    for b in range(4): w[:, i, b, i, b] = -1
    return {**both(x * 2.0 ** 30, u * 2.0 ** 30), "v": d["v"], **weights(rng, w.astype(BF))}
def setup_inputs_odd(rng):
    d = numbers_of(rng)
    x = d["x"].astype(np.float32).reshape(N, 8, 16, C, 4)
    u = d["u"].astype(np.float32).reshape(N, 8, 16, 128, 4)
    for a, n in ((x, C), (u, 128)):
        a[:, :, :8] = (2 * rng.integers(0, 8, (N, 8, 8, n, 4)) + 1) * rng.choice([-1.0, 1.0], (N, 8, 8, n, 4)) * 2.0 ** -16
        a[:, :, 0, :, 0] = rng.choice([1.625, 1.75, 1.875, 1.96875], (N, 8, n))
        a[:, :, 8] = 0
        a[:, :, 8, :, 0] = 1
    w = layers(rng)
    w[:, :, :, :, :, :9] = 0
    for g in range(8): w[:, g, 8, 0, g, 0, 0] = 3
    return {**both(x, u), "v": d["v"], **weights(rng, w)}
def setup_inputs_spread(rng):
    d = setup_inputs(rng)
    d["x"] = wide(rng, N, 128, 4 * C, cols=6)
    return d
def check_inputs(d):
    b = []
    for k in ("x", "u", "v"):
        a = np.abs(d[k].astype(np.float32))
        if not (np.isfinite(a).all() and ((a == 0) | (a >= 2.0 ** -30) & (a <= 2.0 ** 30)).all()): b.append("a value of " + k)
    none, least, most = [emit(mx_ref.quantize(np.full((128, 16), k, np.float32).astype(BF)))[1][0, 0] for k in (0.0, 2.0 ** -30, 2.0 ** 30)]
    for r in range(N):
        if ((d["wc"][r] == 0x7F) | (d["wc"][r] == 0xFF)).any(): b.append("wc: a code that is no number")
        s = mx_ref.live(d["ws"][r])
        if ((s != none) & ((s < least) | (s > most))).any(): b.append("ws: a scale out of range")
    return b
def reference(x, u, v, wc, ws):
    lay = [pk(wc[r], ws[r]) for r in range(N)]
    now = [mx_ref.quantize(x[r]) for r in range(N)]
    stat = [mx_ref.quantize(u[r]) for r in range(N)]
    down, along = np.zeros((N, 8, C), np.int64), np.zeros((N, 8, 128), np.int64)
    for h in STEP:
        sent = []
        for r in range(N):
            own = decode(now[r])
            s = mx_ref.matmul(stat[r], now[r]) + np.float32(0.0)
            down[r] = np.argmax(s.reshape(8, 16, C), axis=1) + 16 * np.arange(8)[:, None]
            along[r] = np.argsort(-s, axis=1, kind="stable")[:, :8].T
            a = gcols(decode(stat[r]).astype(BF), down[r]).astype(np.float32)
            z = mx_ref.quantize(((own + a) * np.float32(0.5)).astype(BF))
            now[r] = mx_ref.quantize(tile([mx_ref.matmul(pick(lay[r], np.arange(128 * b, 128 * b + 128)), z) * np.float32(0.03125) + own[:, b::4] for b in range(4)]))
            sent.append(mx_ref.quantize(gcols(decode(now[r]).astype(BF), along[r])))
        stat = [sent[(r - h) % N] for r in range(N)]
    y, op = np.zeros((N, 128, C), np.float32), np.zeros((N, 8, C + 128), np.float32)
    oc, osc = np.zeros((N, 128, 4 * C), np.uint8), np.zeros((N, 16, C), np.uint8)
    uc, usc = np.zeros((N, 128, 512), np.uint8), np.zeros((N, 16, 128), np.uint8)
    for r in range(N):
        y[r] = mx_ref.matmul(mx_ref.quantize(v[r]), now[r])
        op[r, :, :C] = down[r]
        op[r, :, C:] = along[r]
        oc[r], osc[r] = emit(now[r])
        uc[r], usc[r] = emit(stat[r])
    return {"y": y, "op": op, "oc": oc, "osc": osc, "uc": uc, "usc": usc}

@@ -1,0 +1,411 @@
+from concourse.mybir import dt, AluOpType, ActivationFunctionType
+
+ALU = AluOpType
+ACTF = ActivationFunctionType
+STEP = [1, 2, 4]
+BIG = 1.0e29
+ON_SCALAR = (1, 2, 3, 4)
+TS, XS, RS, VS = "AAAA", "AAVV", "AAVV", "AAVV"
+
+SCRATCH = {
+    "xin": ("sbuf", [128, 1024], "bfloat16"), "uin": ("sbuf", [128, 512], "bfloat16"), "vin": ("sbuf", [128, 512], "bfloat16"),
+    "eh": ("sbuf", [128, 2048], "bfloat16"), "full": ("sbuf", [128, 512], "bfloat16"), "ioe": ("sbuf", [128, 512], "float32"),
+    "iob": ("sbuf", [128, 256], "bfloat16"), "dist": ("sbuf", [128, 512], "float32"),
+    "seg": ("sbuf", [128, 256], "float32"), "top": ("sbuf", [128, 256], "float32"), "ones": ("sbuf", [128, 256], "bfloat16"),
+    "ib": ("sbuf", [128, 16], "int32"), "fb": ("sbuf", [128, 8], "float32"), "iw": ("sbuf", [128, 8], "int32"), "base": ("sbuf", [128, 1], "float32"),
+    "dupl": ("sbuf", [128, 4], "uint16"), "seld": ("sbuf", [128, 2], "uint16"), "seln": ("sbuf", [128, 2], "uint16"),
+    "st": ("sbuf", [128, 256], "float32"), "rd": ("sbuf", [128, 264], "float32"),
+    "qd": ("sbuf", [128, 256], "bfloat16"), "cd": ("sbuf", [128, 256], "bfloat16"),
+    "kc": ("sbuf", [128, 32], "bfloat16"), "kt": ("sbuf", [128, 32], "bfloat16"),
+    "kd": ("sbuf", [128, 64], "bfloat16"), "ko": ("sbuf", [128, 64], "bfloat16"),
+    "offd": ("sbuf", [128, 16], "uint16"), "offn": ("sbuf", [128, 16], "uint16"),
+    "rb": ("sbuf", [128, 8 * 264], "float32"),
+    "db0": ("sbuf", [128, 256], "float32"), "db1": ("sbuf", [128, 256], "float32"),
+    "neb": ("sbuf", [128, 2048], "bfloat16"), "sgb": ("sbuf", [128, 2048], "bfloat16"), "cb": ("sbuf", [128, 2048], "bfloat16"),
+    "junk": ("sbuf", [128, 256], "bfloat16"), "n0": ("sbuf", [128, 1], "float32"),
+    "jn": ("sbuf", [128, 8], "float32"), "jm": ("sbuf", [128, 8], "float32"), "more": ("sbuf", [128, 8], "float32"),
+    "less": ("sbuf", [128, 8], "float32"), "part": ("sbuf", [128, 8], "float32"), "held": ("sbuf", [128, 8], "float32"),
+    "nb": ("sbuf", [128, 32], "float32"), "nt": ("sbuf", [128, 32], "float32"),
+    "nd": ("sbuf", [128, 64], "bfloat16"), "ngo": ("sbuf", [128, 64], "bfloat16"),
+    "du": ("sbuf", [128, 512], "bfloat16"), "tp": ("sbuf", [128, 1024], "bfloat16"), "tr": ("sbuf", [128, 1024], "bfloat16"),
+    "zt": ("sbuf", [128, 1024], "bfloat16"), "xt": ("sbuf", [128, 1024], "bfloat16"), "vt": ("sbuf", [128, 512], "bfloat16"),
+    "opk": ("sbuf", [128, 256], "float32"), "opn": ("sbuf", [128, 128], "float32"), "ysb": ("sbuf", [128, 256], "float32"),
+    "pd": ("psum", [128, 2048], "float32"), "pr": ("psum", [128, 2048], "float32"),
+}
+
+
+def _pair(name, plane, n):
+    SCRATCH[name] = ("sbuf", [128, n], "float8_e4m3fn_x4")
+    SCRATCH[plane] = ("sbuf", [128, n], "uint8")
+
+
+_pair("wq", "wp", 512)
+_pair("ehq", "ehp", 512)
+_pair("vcq", "vcp", 128)
+for _r in range(4):
+    _pair("q%d" % _r, "p%d" % _r, 256)
+    _pair("u%d" % _r, "s%d" % _r, 128)
+for _r in range(3):
+    _pair("zq%d" % _r, "zp%d" % _r, 256)
+    _pair("xl%d" % _r, "xs%d" % _r, 256)
+    SCRATCH["lo%d" % _r] = ("sbuf", [128, 8], "uint16")
+
+SEMAPHORES = ["sv", "sa", "sp", "sg"] + ["%s%d" % (n, r) for n in ("arr", "sent", "lst", "lsent") for r in range(3)] + ["d%d" % k for k in range(24)]
+
+CYC = 0.00083 * 1.25
+WAKE = 0.07
+
+
+def rank_program(g, core, T, topo):
+    rank = T.rank_of(core)
+    if rank is None:
+        return
+    ops = []
+    last_w, readers = {}, {}
+    queue = {"V": g.vector, "A": g.scalar, "P": g.tensor, "G": g, "S": g.sync, "AD": g.scalar}
+    csem = {"V": "sv", "A": "sa", "P": "sp", "G": "sg"}
+    ndma = [0]
+
+    def op(eng, cost, fn, reads=(), writes=(), sem=None, inc=1, extra=0.0):
+        k = len(ops)
+        hard, order = set(), set()
+        for b in reads:
+            if b in last_w:
+                hard.add(last_w[b])
+        for b in writes:
+            for d in ([last_w[b]] if b in last_w else []) + readers.get(b, []):
+                if eng == "P" and ops[d]["eng"] == "P" and b[:2] in ("PD", "PR"):
+                    order.add(d)
+                else:
+                    hard.add(d)
+        for b in reads:
+            readers.setdefault(b, []).append(k)
+        for b in writes:
+            last_w[b] = k
+            readers[b] = []
+        ops.append({"k": k, "eng": eng, "u": "A" if eng == "AD" else eng, "cost": cost, "extra": extra, "fn": fn,
+                    "hard": hard - {k}, "order": order - {k}, "sem": sem, "inc": inc, "w": list(writes)})
+
+    def V(n, fn, reads, writes, cyc=1.0):
+        op("V", max(64, n * cyc) * CYC, fn, reads, writes)
+
+    def GA(n, fn, reads, writes):
+        op("V", 0.05 + n * 1.5 * CYC, fn, reads, writes)
+
+    def A(n, fn, reads, writes, fix=0.06):
+        op("A", fix + n * CYC, fn, reads, writes)
+
+    def AG(n, fn, reads, writes):
+        op("A", 0.065 + n * 1.5 * CYC, fn, reads, writes)
+
+    def bank(b, n=256):
+        return T[b[0]][:, 512 * b[1]:512 * b[1] + n], b[0].upper() + "%d" % b[1]
+
+    def mm(b, lhs, rhs, n, start, stop, reads):
+        out, name = bank(b, n)
+        op("P", (n + 16) * CYC, lambda: g.tensor.matmul_mx(out, lhs[0], lhs[1], rhs[0], rhs[1], start, stop), reads, [name])
+
+    def dma(eng, out, in_, reads, writes, lat=2.2):
+        s = "d%d" % ndma[0]
+        ndma[0] += 1
+        op(eng, 0.08, lambda: queue[eng].dma_start(out, in_), reads, writes, sem=s, inc=16, extra=lat)
+
+    def quant(q, p, t, n, reads, writes):
+        op("V", 0.012 + 0.00022 * 4 * n * 1.25, lambda: g.vector.quantize_mx(q, p, t), reads, writes)
+
+    tt, ts, tc = g.vector.tensor_tensor, g.vector.tensor_scalar, g.vector.tensor_copy
+    scan, act = g.vector.tensor_tensor_scan, g.scalar.activation
+    B4 = range(4)
+
+    def copy(e, o, i, n, reads, writes, scale=1.0):
+        if e == "A":
+            A(n, lambda: act(o, i, ACTF.Copy, scale=scale), reads, writes)
+        elif scale == 1.0:
+            V(n, lambda: tc(o, i), reads, writes)
+        else:
+            V(n, lambda: ts(o, i, scale, None, ALU.mult), reads, writes)
+
+    dma("S", T.xin[:], T.x[:], [], ["xin"])
+    dma("AD", T.uin[:], T.u[:], [], ["uin"])
+    dma("S", T.wq[:].bitcast(dt.uint8), T.wc[:], [], ["wq"])
+    dma("AD", T.wp[:], T.ws[:], [], ["wp"])
+    dma("S", T.vin[:], T.v[:], [], ["vin"])
+
+    op("G", 0.2, lambda: g.iota(T.iw[:, 0:4], [[0, 4]], 0, 1), [], ["iw0"])
+    op("G", 1.2, lambda: g.iota(T.ioe[:], [[1, 512]], 0, -4, allow_small_or_imprecise_dtypes=True), [], ["ioe"])
+    V(256, lambda: g.vector.memset(T.full[:], 32.0), [], ["full"])
+    op("G", 1.3, lambda: g.affine_select(T.eh[:, 1536:2048], T.full[:], [[-1, 512]], ALU.is_equal, 0.0, 3, 4), ["full"], ["eh3"])
+    op("G", 0.2, lambda: g.iota(T.iw[:, 4:8], [[16, 2], [0, 2]], 0, 0), [], ["iw1"])
+    op("G", 0.7, lambda: g.iota(T.iob[:], [[1, 256]], 0, 0, allow_small_or_imprecise_dtypes=True), [], ["iob"])
+    A(512, lambda: act(T.dist[:], T.ioe[:], ACTF.Abs, bias=-2.0), ["ioe"], ["dist"])
+    A(512, lambda: act(T.eh[:, 1024:1536], T.dist[:], ACTF.Relu, bias=32.0, scale=-32.0), ["dist"], ["eh2"])
+    for b in (0, 1):
+        V(512, lambda b=b: ts(T.eh[:, 512 * b:512 * b + 512], T.ioe[:], float(b), 32.0, ALU.is_equal, ALU.mult), ["ioe"], ["eh%d" % b])
+    quant(T.ehq[:], T.ehp[:], T.eh[:], 512, ["eh%d" % b for b in B4], ["ehq"])
+
+    def col(k):
+        return T.ib[:, k:k + 1]
+
+    def fcol(k):
+        return T.fb[:, k:k + 1]
+
+    def bit(k, s1, o1, s2=None, o2=None):
+        if o2 is None:
+            V(1, lambda: ts(col(k), T.iw[:, 0:1], s1, None, o1), ["iw0"], ["ib%d" % k])
+        else:
+            V(1, lambda: ts(col(k), T.iw[:, 0:1], s1, s2, o1, o2), ["iw0"], ["ib%d" % k])
+    bit(0, 15, ALU.bitwise_and)
+    bit(1, 1, ALU.bitwise_and)
+    bit(2, 4, ALU.logical_shift_right, 1, ALU.bitwise_and)
+    bit(3, 7, ALU.bitwise_and, 1, ALU.logical_shift_right)
+    bit(4, 5, ALU.logical_shift_right)
+    bit(5, 4, ALU.logical_shift_right)
+    V(1, lambda: tc(fcol(0), col(0)), ["ib0"], ["fb0"])
+    V(1, lambda: ts(T.dupl[:], T.iw[:, 4:8], fcol(0), None, ALU.add), ["fb0", "iw1"], ["dupl"])
+    V(1, lambda: tt(fcol(1), col(0), col(2), ALU.add), ["ib0", "ib2"], ["fb1"])
+    V(1, lambda: ts(T.seld[:, 0:1], col(1), 31.0, fcol(1), ALU.mult, ALU.add), ["ib1", "fb1"], ["seld"])
+    V(1, lambda: tc(fcol(2), col(5)), ["ib5"], ["fb2"])
+    V(1, lambda: ts(T.base[:], col(5), 16.0, 15.0, ALU.mult, ALU.add), ["ib5"], ["base"])
+    V(1, lambda: tt(col(7), col(3), col(4), ALU.subtract), ["ib3", "ib4"], ["ib7"])
+    V(1, lambda: ts(col(8), col(7), 3, None, ALU.bitwise_and), ["ib7"], ["ib8"])
+    V(1, lambda: ts(fcol(3), col(8), 8.0, fcol(2), ALU.mult, ALU.add), ["ib8", "fb2"], ["fb3"])
+    V(1, lambda: ts(T.seln[:, 0:1], col(1), 32.0, fcol(3), ALU.mult, ALU.add), ["ib1", "fb3"], ["seln"])
+    A(256, lambda: act(T.top[:], T.ioe[:, 0:256], ACTF.Identity, bias=BIG, scale=0.0), ["ioe"], ["top"])
+    A(256, lambda: act(T.seg[:], T.ioe[:, 0:256], ACTF.Identity, bias=BIG, scale=0.0), ["ioe"], ["seg0"])
+    A(16, lambda: act(T.seg[:, 0:256:16], T.ioe[:, 0:16], ACTF.Identity, bias=-BIG, scale=0.0), ["ioe", "seg0"], ["seg0"])
+    A(256, lambda: act(T.ones[:], T.ioe[:, 0:256], ACTF.Identity, bias=1.0, scale=0.0), ["ioe"], ["ones"])
+    V(8, lambda: g.vector.memset(T.rb[:, 0:8 * 264:264], -BIG), [], ["rbi"])
+    V(1, lambda: g.vector.memset(T.rd[:, 0:1], 0.0), [], ["rd0"])
+    V(16, lambda: g.vector.memset(T.kc[:], 0.0), [], ["kc"])
+
+    def W(name, b):
+        return (T[name + "q"][:, 128 * b:128 * b + 128], T[name + "p"][:, 128 * b:128 * b + 128])
+
+    quant(T.q0[:], T.p0[:], T.xin[:], 256, ["xin"], ["q0"])
+    quant(T.u0[:], T.s0[:], T.uin[:], 128, ["uin"], ["u0"])
+
+    def unpack(q, p, to, at, how, scale):
+        for b in B4:
+            mm((at, b), W("eh", b), (T[q][:], T[p][:]), 256, True, True, ["ehq", q])
+        for b in B4:
+            i, bn = bank((at, b))
+            copy(how[b], T[to][:, 256 * b:256 * b + 256], i, 256, [], ["%s%d" % (to, b), bn], scale)
+
+    unpack("q0", "p0", "tp", "pr", TS, 0.015625)
+    for r, h in enumerate(STEP):
+        qn, un, q2, p2, u2, s2 = "q%d" % r, "u%d" % r, "q%d" % (r + 1), "p%d" % (r + 1), "u%d" % (r + 1), "s%d" % (r + 1)
+        Q, U = (T[qn][:], T["p%d" % r][:]), (T[un][:], T["s%d" % r][:])
+        Z = (T["zq%d" % r][:], T["zp%d" % r][:])
+        dst = T.cores[(rank + h) % len(T.cores)]
+        rid, pid, _ = topo.addr(dst)
+        m, ne = topo.mask(core, dst), len(topo.engines(core, dst))
+
+        def send(cost, lat, moves, reads, writes, arr, sent, rid=rid, pid=pid, m=m, ne=ne):
+            def go():
+                for o, i in moves:
+                    g.remote_dma(o, i, T.sem[arr], T.sem[sent], pid, rid, m)
+            op("G", cost, go, reads, [sent], sem=sent, inc=len(moves) * ne)
+            op("N", lat, None, [sent], writes, sem=arr, inc=len(moves) * ne)
+
+        mm(("pd", 0), U, Q, 256, True, True, [qn, un])
+        mm(("pd", 1), U, Q, 256, True, True, [qn, un])
+        for b in B4:
+            at = ("pd", 2 + b % 2) if r == 0 else ("pr", b)
+            mm(at, W("eh", b), U, 128, True, True, ["ehq", un])
+            i, bn = bank(at, 128)
+            copy("A", T.du[:, 128 * b:128 * b + 128], i, 128, [], ["du%d" % b, bn], 0.015625)
+        for b in B4:
+            mm(("pr", b), W("eh", b), Q, 256, True, False, ["ehq", qn])
+        V(256, lambda: g.vector.transpose(T.st[:], T.pd[:, 0:256]), [], ["st", "PD0"])
+        V(256, lambda: scan(T.rd[:, 1:257], T.seg[:], T.st[:], 0.0, ALU.min, ALU.max), ["seg0", "st"], ["rd"])
+        V(256, lambda: tt(T.qd[:], T.rd[:, 0:256], T.st[:], ALU.is_ge), ["rd", "rd0", "st"], ["qd"], 2.0)
+        V(256, lambda: scan(T.cd[:], T.qd[:], T.qd[:], 0.0, ALU.mult, ALU.add), ["qd"], ["cd"], 0.5)
+        V(16, lambda: ts(T.kc[:, 0:16], T.cd[:, 15:256:16], 15.0, None, ALU.min), ["cd"], ["kc"])
+        V(32, lambda: g.vector.transpose(T.kt[:], T.kc[:]), ["kc"], ["kt"])
+        GA(64, lambda: tc(T.kd[:], T.kt[:, 0:32].indirect(T.dupl[:, 0:4])), ["kt", "dupl"], ["kd"])
+        V(64, lambda: g.vector.transpose(T.ko[:], T.kd[:]), ["kd"], ["ko"])
+        GA(16, lambda: ts(T.offd[:], T.ko[:, 0:64].indirect(T.seld[:, 0:1]), -1.0, T.base[:], ALU.mult, ALU.add), ["ko", "seld", "base"], ["offd"])
+        for b in B4:
+            GA(256, lambda b=b: tt(T.zt[:, b:1024:4], T.du[:, 128 * b:128 * b + 128].indirect(T.offd[:, 0:16]), T.tp[:, 256 * b:256 * b + 256], ALU.add),
+               ["du%d" % b, "offd", "tp%d" % b], ["zt%d" % b])
+        quant(Z[0], Z[1], T.zt[:], 256, ["zt%d" % b for b in B4], ["zq%d" % r])
+        for b in B4:
+            mm(("pr", b), W("w", b), Z, 256, False, True, ["wq", "wp", "zq%d" % r])
+        for b in B4:
+            i, bn = bank(("pr", b))
+            copy(XS[b], T.xt[:, b:1024:4], i, 256, [], ["xt%d" % b, bn], 0.03125)
+        quant(T[q2][:], T[p2][:], T.xt[:], 256, ["xt%d" % b for b in B4], [q2])
+        send(1.0, 3.0, [(T["xl%d" % r][:].bitcast(dt.uint8), T[q2][:].bitcast(dt.uint8)), (T["xs%d" % r][:], T[p2][:])],
+             [q2], ["xl%d" % r], "arr%d" % r, "sent%d" % r)
+        for k in range(8):
+            o, kk = 264 * k, slice(k, k + 1)
+            run, v, w = T.rb[:, o + 1:o + 257], T.rb[:, o + 256:o + 257], T.rb[:, o - 8:o - 7]
+            if k == 0:
+                V(256, lambda run=run: scan(run, T.top[:], T.pd[:, 0:256], -2.0 * BIG, ALU.min, ALU.max), ["top"], ["rb0", "PD0"])
+                A(256, lambda run=run, v=v: act(T.junk[:], run, ACTF.Sign, bias=v, scale=-1.0, accum_out=T.n0[:]), ["rb0"], ["junk", "n0"], 0.1)
+                A(1, lambda: act(T.nb[:, 0:1], T.n0[:], ACTF.Identity, bias=-256.0, scale=2.0), ["n0"], ["nb0"])
+                continue
+            dk, ok = "db%d" % (k % 2), "db%d" % ((k - 1) % 2)
+            out, old, shifted = T[dk][:], T[ok][:], T.rb[:, o - 264:o - 8]
+            if k == 1:
+                V(256, lambda out=out, x=shifted: scan(out, x, T.pd[:, 0:256], -2.0 * BIG, ALU.max, ALU.min), ["rb0", "rbi"], [dk, "PD0"])
+            else:
+                V(256, lambda out=out, x=shifted, old=old: scan(out, x, old, -2.0 * BIG, ALU.max, ALU.min), ["rb%d" % (k - 1), "rbi", ok], [dk])
+            V(256, lambda out=out, run=run: scan(run, out, out, -2.0 * BIG, ALU.max, ALU.max), [dk, "rbi"], ["rb%d" % k])
+            e, c, f = [T[x][:, 256 * k:256 * k + 256] for x in ("neb", "cb", "sgb")]
+            if k in ON_SCALAR:
+                A(256, lambda f=f, v=v, kk=kk: act(f, T.pd[:, 512:768], ACTF.Sign, bias=v, scale=-1.0, accum_out=T.less[:, kk]),
+                  ["rb%d" % k], ["sgb%d" % k, "less%d" % k, "PD1"], 0.08)
+                A(256, lambda f=f, e=e, kk=kk: act(e, f, ACTF.Abs, accum_out=T.more[:, kk]), ["sgb%d" % k], ["neb%d" % k, "more%d" % k], 0.08)
+                A(1, lambda k=k, kk=kk: act(T.part[:, kk], T.less[:, kk], ACTF.Identity, bias=k + 0.5, scale=0.5), ["less%d" % k], ["part%d" % k])
+                A(1, lambda kk=kk: act(T.held[:, kk], T.more[:, kk], ACTF.Identity, bias=T.part[:, kk], scale=-0.5),
+                  ["more%d" % k, "part%d" % k], ["held%d" % k])
+                first, half, need = 0.0, T.held[:, kk], []
+                if k < 7 and k + 1 not in ON_SCALAR:
+                    A(1, lambda kk=kk: act(T.jm[:, kk], T.held[:, kk], ACTF.Identity, bias=0.5), ["held%d" % k], ["jm%d" % k])
+            else:
+                V(256, lambda e=e, v=v: ts(e, T.pd[:, 0:256], v, None, ALU.not_equal), ["rb%d" % k], ["neb%d" % k, "PD0"])
+                V(1, lambda v=v, w=w, k=k, kk=kk: ts(T.jn[:, kk], v, w, T.jm[:, k - 1:k], ALU.is_equal, ALU.mult),
+                  ["rb%d" % k, "rb%d" % (k - 1), "jm%d" % (k - 1)], ["jn%d" % k])
+                if k < 7 and k + 1 not in ON_SCALAR:
+                    A(1, lambda kk=kk: act(T.jm[:, kk], T.jn[:, kk], ACTF.Identity, bias=1.0), ["jn%d" % k], ["jm%d" % k])
+                first, half, need = T.jn[:, kk], 0.5, ["jn%d" % k]
+            V(256, lambda e=e, c=c, first=first: scan(c, e, T.ones[:], first, ALU.add, ALU.subtract), ["neb%d" % k, "ones"] + need, ["cb%d" % k], 0.5)
+            A(256, lambda c=c, kk=kk, half=half: act(T.junk[:], c, ACTF.Sign, bias=half, accum_out=T.nb[:, kk]),
+              ["cb%d" % k] + ([] if need else ["held%d" % k]), ["junk", "nb%d" % k], 0.1)
+        NB = ["nb%d" % k for k in range(8)]
+        for q in B4:
+            copy("VA"[q % 2], T.nb[32 * q:32 * q + 32, 8:16], T.nb[32 * ((q + 1) % 4):32 * ((q + 1) % 4) + 32, 0:8], 8, NB, ["nx%d" % q])
+        NX = NB + ["nx%d" % q for q in B4]
+        copy("V", T.nb[0:64, 16:32], T.nb[64:128, 0:16], 16, NX, ["ny0"])
+        copy("A", T.nb[64:128, 16:32], T.nb[0:64, 0:16], 16, NX, ["ny1"])
+        V(32, lambda: g.vector.transpose(T.nt[:], T.nb[:]), NX + ["ny0", "ny1"], ["nt"])
+        GA(64, lambda: tc(T.nd[:], T.nt[:, 0:32].indirect(T.dupl[:, 0:4])), ["nt", "dupl"], ["nd"])
+        V(64, lambda: g.vector.transpose(T.ngo[:], T.nd[:]), ["nd"], ["ngo"])
+        GA(16, lambda: ts(T.offn[:], T.ngo[:, 0:64].indirect(T.seln[:, 0:1]), 0.5, 128.0, ALU.mult, ALU.add), ["ngo", "seln"], ["offn"])
+        send(0.5, 1.5, [(T["lo%d" % r][:], T.offn[:, 0:8])], ["offn"], ["lo%d" % r], "lst%d" % r, "lsent%d" % r)
+        unpack("xl%d" % r, "xs%d" % r, "tr", "pr", RS, 0.03125)
+        if r < 2:
+            unpack(q2, p2, "tp", "pd", TS, 0.015625)
+        for b in B4:
+            o, i = T.vt[:, b:512:4], T.tr[:, 256 * b:256 * b + 256].indirect(T["lo%d" % r][:, 0:8])
+            if VS[b] == "A":
+                AG(128, lambda o=o, i=i: act(o, i, ACTF.Copy), ["tr%d" % b, "lo%d" % r], ["vt%d" % b])
+            else:
+                GA(128, lambda o=o, i=i: tc(o, i), ["tr%d" % b, "lo%d" % r], ["vt%d" % b])
+        quant(T[u2][:], T[s2][:], T.vt[:], 128, ["vt%d" % b for b in B4], [u2])
+        if r == 0:
+            quant(T.vcq[:], T.vcp[:], T.vin[:], 128, ["vin"], ["vcq"])
+    mm(("pd", 2), (T.vcq[:], T.vcp[:]), (T.q3[:], T.p3[:]), 256, True, True, ["vcq", "q3"])
+    copy("A", T.ysb[:], bank(("pd", 2))[0], 256, [], ["ysb", "PD2"])
+    dma("S", T.oc[:], T.q3[:].bitcast(dt.uint8), ["q3"], [])
+    for k in B4:
+        dma("S", T.osc[4 * k:4 * k + 4, :], T.p3[32 * k:32 * k + 4, :], ["q3"], [])
+    dma("S", T.y[:], T.ysb[:], ["ysb"], [])
+    AG(256, lambda: act(T.opk[:], T.iob[:].indirect(T.offd[:, 0:16]), ACTF.Copy), ["iob", "offd"], ["opk"])
+    AG(128, lambda: act(T.opn[:], T.iob[:].indirect(T.offn[:, 0:8]), ACTF.Copy), ["iob", "offn"], ["opn"])
+    dma("S", T["op"][:, 0:256], T.opk[0:128:16, :], ["opk"], [])
+    dma("S", T["op"][:, 256:384], T.opn[0:128:16, :], ["opn"], [])
+    dma("S", T.uc[:], T.u3[:].bitcast(dt.uint8), ["u3"], [])
+    for k in B4:
+        dma("AD" if k % 2 else "S", T.usc[4 * k:4 * k + 4, :], T.s3[32 * k:32 * k + 4, :], ["u3"], [])
+    plan_and_emit(g, T, ops, queue, csem)
+
+
+TRIES, FOUND = 700, {}
+ASSUMED = [(1.0, 0.07, 0.0), (0.8, 0.07, 0.0), (1.0, 0.2, 0.0), (1.2, 0.07, 1.0), (0.8, 0.07, 2.0), (1.0, 0.03, 0.0)]
+
+
+def find_order(ops):
+    n = len(ops)
+    unit, cost, extra, hard = [o["u"] for o in ops], [o["cost"] for o in ops], [o["extra"] for o in ops], [sorted(o["hard"]) for o in ops]
+    need = [len(o["hard"] | o["order"]) for o in ops]
+    succ = [[] for _ in range(n)]
+    for o in ops:
+        for d in o["hard"] | o["order"]:
+            succ[d].append(o["k"])
+    tail = [0.0] * n
+    for k in range(n - 1, -1, -1):
+        tail[k] = cost[k] + extra[k] + max([tail[s] + WAKE for s in succ[k]] + [0.0])
+
+    def plan(key):
+        left, free, end, seq = list(need), {u: 0.0 for u in unit}, [0.0] * n, []
+        ready = {k: 0.0 for k in range(n) if left[k] == 0}
+        while ready:
+            est = [(max(t, free[unit[k]]), k) for k, t in ready.items()]
+            lo = min(est)[0] + 0.06
+            t, k = max((e for e in est if e[0] <= lo), key=lambda e: (key[e[1]], -e[1]))
+            free[unit[k]] = t + cost[k]
+            end[k] = t + cost[k] + extra[k]
+            seq.append(k)
+            del ready[k]
+            for s in succ[k]:
+                left[s] -= 1
+                if left[s] == 0:
+                    ready[s] = max([end[d] + WAKE for d in hard[s]] + [0.0])
+        return seq
+
+    def ends(seq):
+        total = 0.0
+        for f, wake, late in ASSUMED:
+            free, end = {u: 0.0 for u in unit}, [0.0] * n
+            for k in seq:
+                u = unit[k]
+                t = 0.0 if u == "N" else free[u]
+                for d in hard[k]:
+                    if end[d] + wake > t:
+                        t = end[d] + wake
+                t += late + cost[k] if u == "N" else cost[k] * f if u in "VAP" else cost[k]
+                free[u] = t
+                end[k] = t + extra[k]
+            total += max(end)
+        return total
+
+    state = [12345]
+
+    def rnd(m):
+        state[0] = (state[0] * 1103515245 + 12345) % 2147483648
+        return (state[0] >> 8) % m
+    key = tail
+    best = plan(key)
+    least = ends(best)
+    for i in range(TRIES):
+        trial = list(key)
+        for _ in range(n if i < 40 else (2, 5, 12)[rnd(3)]):
+            trial[_ if i < 40 else rnd(n)] += (rnd(1000) / 1000.0) * 0.4 if i < 40 else (rnd(1000) + rnd(1000) - 1000) / 700.0
+        seq = plan(trial)
+        e = ends(seq)
+        if e < least:
+            best, least, key = seq, e, trial
+    return best
+
+
+def plan_and_emit(g, T, ops, queue, csem):
+    if len(ops) not in FOUND:
+        FOUND[len(ops)] = find_order(ops)
+    count, clock, after = {}, {}, {}
+    for i, k in enumerate(FOUND[len(ops)]):
+        o = ops[k]
+        known = clock.setdefault(o["u"], {})
+        need = {}
+        for d in sorted(o["hard"], key=lambda d: -after[d][2]):
+            s, v, _, seen = after[d]
+            if known.get(s, 0) >= v:
+                continue
+            need[s] = max(need.get(s, 0), v)
+            for a, b in seen.items():
+                known[a] = max(known.get(a, 0), b)
+            known[s] = max(known.get(s, 0), v)
+        if o["fn"] is not None:
+            for s, v in need.items():
+                queue[o["eng"]].wait_ge(T.sem[s], v)
+        s = o["sem"] or csem[o["eng"]]
+        count[s] = count.get(s, 0) + o["inc"]
+        if o["fn"] is not None:
+            c = o["fn"]()
+            if c is not None:
+                c.then_inc(T.sem[s], o["inc"])
+        after[k] = (s, count[s], i, dict(known) if o["fn"] is not None else {})
+    for s, v in count.items():
+        if clock["G"].get(s, 0) < v:
+            g.wait_ge(T.sem[s], v)

@@ -4,30 +4,25 @@ ALU = AluOpType
 ACTF = ActivationFunctionType
 STEP = [1, 2, 4]
 BIG = 1.0e29
-ON_SCALAR = (1, 2, 3, 4)
-TS, XS, RS, VS = "AAAA", "AAVV", "AAVV", "AAVV"
+ZS = "AAVV"
+TS, XS, RS, VS, QS = "AAAA", "AAAV", "AAVV", "AAVV", "VAVA"
 
 SCRATCH = {
     "xin": ("sbuf", [128, 1024], "bfloat16"), "uin": ("sbuf", [128, 512], "bfloat16"), "vin": ("sbuf", [128, 512], "bfloat16"),
-    "eh": ("sbuf", [128, 2048], "bfloat16"), "full": ("sbuf", [128, 512], "bfloat16"), "ioe": ("sbuf", [128, 512], "float32"),
-    "iob": ("sbuf", [128, 256], "bfloat16"), "dist": ("sbuf", [128, 512], "float32"),
-    "seg": ("sbuf", [128, 256], "float32"), "top": ("sbuf", [128, 256], "float32"), "ones": ("sbuf", [128, 256], "bfloat16"),
+    "full": ("sbuf", [128, 516], "bfloat16"), "ef": ("sbuf", [128, 516], "bfloat16"), "eh": ("sbuf", [128, 516], "bfloat16"),
+    "iob": ("sbuf", [128, 256], "bfloat16"), "k0": ("sbuf", [128, 256], "float16"), "odd": ("sbuf", [128, 512], "bfloat16"),
+    "seg": ("sbuf", [128, 256], "float32"), "top": ("sbuf", [128, 256], "float32"),
     "ib": ("sbuf", [128, 16], "int32"), "fb": ("sbuf", [128, 8], "float32"), "iw": ("sbuf", [128, 8], "int32"), "base": ("sbuf", [128, 1], "float32"),
-    "dupl": ("sbuf", [128, 4], "uint16"), "seld": ("sbuf", [128, 2], "uint16"), "seln": ("sbuf", [128, 2], "uint16"),
+    "seld": ("sbuf", [128, 2], "uint16"), "seln": ("sbuf", [128, 2], "uint16"),
     "st": ("sbuf", [128, 256], "float32"), "rd": ("sbuf", [128, 264], "float32"),
-    "qd": ("sbuf", [128, 256], "bfloat16"), "cd": ("sbuf", [128, 256], "bfloat16"),
-    "kc": ("sbuf", [128, 32], "bfloat16"), "kt": ("sbuf", [128, 32], "bfloat16"),
-    "kd": ("sbuf", [128, 64], "bfloat16"), "ko": ("sbuf", [128, 64], "bfloat16"),
+    "qd": ("sbuf", [128, 256], "bfloat16"), "cd": ("sbuf", [128, 544], "bfloat16"), "kt": ("sbuf", [128, 64], "bfloat16"),
     "offd": ("sbuf", [128, 16], "uint16"), "offn": ("sbuf", [128, 16], "uint16"),
-    "rb": ("sbuf", [128, 8 * 264], "float32"),
-    "db0": ("sbuf", [128, 256], "float32"), "db1": ("sbuf", [128, 256], "float32"),
-    "neb": ("sbuf", [128, 2048], "bfloat16"), "sgb": ("sbuf", [128, 2048], "bfloat16"), "cb": ("sbuf", [128, 2048], "bfloat16"),
-    "junk": ("sbuf", [128, 256], "bfloat16"), "n0": ("sbuf", [128, 1], "float32"),
-    "jn": ("sbuf", [128, 8], "float32"), "jm": ("sbuf", [128, 8], "float32"), "more": ("sbuf", [128, 8], "float32"),
-    "less": ("sbuf", [128, 8], "float32"), "part": ("sbuf", [128, 8], "float32"), "held": ("sbuf", [128, 8], "float32"),
-    "nb": ("sbuf", [128, 32], "float32"), "nt": ("sbuf", [128, 32], "float32"),
-    "nd": ("sbuf", [128, 64], "bfloat16"), "ngo": ("sbuf", [128, 64], "bfloat16"),
+    "rb": ("sbuf", [128, 8 * 264], "float32"), "kb": ("sbuf", [128, 8 * 264], "float16"),
+    "sg": ("sbuf", [128, 768], "bfloat16"), "k1": ("sbuf", [128, 256], "float16"), "k2": ("sbuf", [128, 256], "float16"),
+    "ki": ("sbuf", [128, 512], "float16"), "kk": ("sbuf", [128, 512], "float16"), "fl": ("sbuf", [128, 8], "int32"),
+    "nb": ("sbuf", [128, 64], "bfloat16"), "nt": ("sbuf", [128, 64], "bfloat16"),
     "du": ("sbuf", [128, 512], "bfloat16"), "tp": ("sbuf", [128, 1024], "bfloat16"), "tr": ("sbuf", [128, 1024], "bfloat16"),
+    "ag": ("sbuf", [128, 1024], "bfloat16"),
     "zt": ("sbuf", [128, 1024], "bfloat16"), "xt": ("sbuf", [128, 1024], "bfloat16"), "vt": ("sbuf", [128, 512], "bfloat16"),
     "opk": ("sbuf", [128, 256], "float32"), "opn": ("sbuf", [128, 128], "float32"), "ysb": ("sbuf", [128, 256], "float32"),
     "pd": ("psum", [128, 2048], "float32"), "pr": ("psum", [128, 2048], "float32"),
@@ -41,6 +36,7 @@ def _pair(name, plane, n):
 
 _pair("wq", "wp", 512)
 _pair("ehq", "ehp", 512)
+_pair("efq", "efp", 512)
 _pair("vcq", "vcp", 128)
 for _r in range(4):
     _pair("q%d" % _r, "p%d" % _r, 256)
@@ -132,16 +128,13 @@ def rank_program(g, core, T, topo):
     dma("S", T.vin[:], T.v[:], [], ["vin"])
 
     op("G", 0.2, lambda: g.iota(T.iw[:, 0:4], [[0, 4]], 0, 1), [], ["iw0"])
-    op("G", 1.2, lambda: g.iota(T.ioe[:], [[1, 512]], 0, -4, allow_small_or_imprecise_dtypes=True), [], ["ioe"])
-    V(256, lambda: g.vector.memset(T.full[:], 32.0), [], ["full"])
-    op("G", 1.3, lambda: g.affine_select(T.eh[:, 1536:2048], T.full[:], [[-1, 512]], ALU.is_equal, 0.0, 3, 4), ["full"], ["eh3"])
-    op("G", 0.2, lambda: g.iota(T.iw[:, 4:8], [[16, 2], [0, 2]], 0, 0), [], ["iw1"])
-    op("G", 0.7, lambda: g.iota(T.iob[:], [[1, 256]], 0, 0, allow_small_or_imprecise_dtypes=True), [], ["iob"])
-    A(512, lambda: act(T.dist[:], T.ioe[:], ACTF.Abs, bias=-2.0), ["ioe"], ["dist"])
-    A(512, lambda: act(T.eh[:, 1024:1536], T.dist[:], ACTF.Relu, bias=32.0, scale=-32.0), ["dist"], ["eh2"])
-    for b in (0, 1):
-        V(512, lambda b=b: ts(T.eh[:, 512 * b:512 * b + 512], T.ioe[:], float(b), 32.0, ALU.is_equal, ALU.mult), ["ioe"], ["eh%d" % b])
-    quant(T.ehq[:], T.ehp[:], T.eh[:], 512, ["eh%d" % b for b in B4], ["ehq"])
+    V(258, lambda: g.vector.memset(T.full[:], 0.5), [], ["full"])
+    op("G", 1.05, lambda: g.affine_select(T.eh[:], T.full[:], [[-1, 516]], ALU.is_equal, 0.0, 3, 4), ["full"], ["eh"])
+    op("G", 0.6, lambda: g.iota(T.iob[:], [[1, 256]], 0, 0, allow_small_or_imprecise_dtypes=True), [], ["iob"])
+    A(516, lambda: act(T.ef[:], T.eh[:], ACTF.Copy, scale=64.0), ["eh"], ["ef"])
+    for e in ("eh", "ef"):
+        for b in B4:
+            quant(T[e + "q"][:, 128 * b:128 * b + 128], T[e + "p"][:, 128 * b:128 * b + 128], T[e][:, 3 - b:515 - b], 128, [e], ["%sq%d" % (e, b)])
 
     def col(k):
         return T.ib[:, k:k + 1]
@@ -149,34 +142,41 @@ def rank_program(g, core, T, topo):
     def fcol(k):
         return T.fb[:, k:k + 1]
 
-    def bit(k, s1, o1, s2=None, o2=None):
+    def bit(k, src, name, s1, o1, s2=None, o2=None):
         if o2 is None:
-            V(1, lambda: ts(col(k), T.iw[:, 0:1], s1, None, o1), ["iw0"], ["ib%d" % k])
+            V(1, lambda: ts(col(k), src, s1, None, o1), [name], ["ib%d" % k])
         else:
-            V(1, lambda: ts(col(k), T.iw[:, 0:1], s1, s2, o1, o2), ["iw0"], ["ib%d" % k])
-    bit(0, 15, ALU.bitwise_and)
-    bit(1, 1, ALU.bitwise_and)
-    bit(2, 4, ALU.logical_shift_right, 1, ALU.bitwise_and)
-    bit(3, 7, ALU.bitwise_and, 1, ALU.logical_shift_right)
-    bit(4, 5, ALU.logical_shift_right)
-    bit(5, 4, ALU.logical_shift_right)
-    V(1, lambda: tc(fcol(0), col(0)), ["ib0"], ["fb0"])
-    V(1, lambda: ts(T.dupl[:], T.iw[:, 4:8], fcol(0), None, ALU.add), ["fb0", "iw1"], ["dupl"])
-    V(1, lambda: tt(fcol(1), col(0), col(2), ALU.add), ["ib0", "ib2"], ["fb1"])
-    V(1, lambda: ts(T.seld[:, 0:1], col(1), 31.0, fcol(1), ALU.mult, ALU.add), ["ib1", "fb1"], ["seld"])
-    V(1, lambda: tc(fcol(2), col(5)), ["ib5"], ["fb2"])
+            V(1, lambda: ts(col(k), src, s1, s2, o1, o2), [name], ["ib%d" % k])
+    p = T.iw[:, 0:1]
+    bit(0, p, "iw0", 14, ALU.bitwise_and)
+    bit(1, p, "iw0", 1, ALU.bitwise_and)
+    bit(2, p, "iw0", 4, ALU.logical_shift_right, 1, ALU.bitwise_and)
+    bit(3, p, "iw0", 7, ALU.bitwise_and, 1, ALU.logical_shift_right)
+    bit(4, p, "iw0", 5, ALU.logical_shift_right)
+    bit(5, p, "iw0", 4, ALU.logical_shift_right)
+    V(1, lambda: tt(col(6), col(1), col(2), ALU.not_equal), ["ib1", "ib2"], ["ib6"])
+    V(1, lambda: tt(col(7), col(0), col(2), ALU.add), ["ib0", "ib2"], ["ib7"])
+    V(1, lambda: ts(fcol(0), col(7), -15.0, 497.0, ALU.mult, ALU.add), ["ib7"], ["fb0"])
+    V(1, lambda: ts(fcol(1), col(7), 16.0, 15.0, ALU.mult, ALU.add), ["ib7"], ["fb1"])
+    V(1, lambda: ts(T.seld[:, 0:1], col(6), fcol(0), fcol(1), ALU.mult, ALU.add), ["ib6", "fb0", "fb1"], ["seld"])
     V(1, lambda: ts(T.base[:], col(5), 16.0, 15.0, ALU.mult, ALU.add), ["ib5"], ["base"])
-    V(1, lambda: tt(col(7), col(3), col(4), ALU.subtract), ["ib3", "ib4"], ["ib7"])
-    V(1, lambda: ts(col(8), col(7), 3, None, ALU.bitwise_and), ["ib7"], ["ib8"])
-    V(1, lambda: ts(fcol(3), col(8), 8.0, fcol(2), ALU.mult, ALU.add), ["ib8", "fb2"], ["fb3"])
-    V(1, lambda: ts(T.seln[:, 0:1], col(1), 32.0, fcol(3), ALU.mult, ALU.add), ["ib1", "fb3"], ["seln"])
-    A(256, lambda: act(T.top[:], T.ioe[:, 0:256], ACTF.Identity, bias=BIG, scale=0.0), ["ioe"], ["top"])
-    A(256, lambda: act(T.seg[:], T.ioe[:, 0:256], ACTF.Identity, bias=BIG, scale=0.0), ["ioe"], ["seg0"])
-    A(16, lambda: act(T.seg[:, 0:256:16], T.ioe[:, 0:16], ACTF.Identity, bias=-BIG, scale=0.0), ["ioe", "seg0"], ["seg0"])
-    A(256, lambda: act(T.ones[:], T.ioe[:, 0:256], ACTF.Identity, bias=1.0, scale=0.0), ["ioe"], ["ones"])
+    V(1, lambda: tt(col(8), col(3), col(4), ALU.subtract), ["ib3", "ib4"], ["ib8"])
+    bit(9, col(8), "ib8", 1, ALU.bitwise_and)
+    bit(10, col(8), "ib8", 2, ALU.bitwise_and)
+    V(1, lambda: tc(fcol(2), col(5)), ["ib5"], ["fb2"])
+    V(1, lambda: ts(fcol(3), col(9), 16.0, fcol(2), ALU.mult, ALU.add), ["ib9", "fb2"], ["fb3"])
+    V(1, lambda: ts(fcol(4), col(10), 4.0, fcol(3), ALU.mult, ALU.add), ["ib10", "fb3"], ["fb4"])
+    V(1, lambda: ts(T.seln[:, 0:1], col(6), 32.0, fcol(4), ALU.mult, ALU.add), ["ib6", "fb4"], ["seln"])
+    A(256, lambda: act(T.top[:], T.iob[:], ACTF.Identity, bias=BIG, scale=0.0), ["iob"], ["top"])
+    A(256, lambda: act(T.seg[:], T.iob[:], ACTF.Identity, bias=BIG, scale=0.0), ["iob"], ["seg0"])
+    A(16, lambda: act(T.seg[:, 0:256:16], T.iob[:, 0:16], ACTF.Identity, bias=-BIG, scale=0.0), ["iob", "seg0"], ["seg0"])
+    A(256, lambda: act(T.odd[:, 0:512:2], T.iob[:], ACTF.Identity, bias=0.0, scale=0.0), ["iob"], ["odd0"])
+    A(256, lambda: act(T.odd[:, 1:512:2], T.iob[:], ACTF.Identity, bias=1.0, scale=0.0), ["iob"], ["odd1"])
+    A(256, lambda: act(T.cd[:, 256:512], T.iob[:], ACTF.Copy), ["iob"], ["cd0"])
+    V(128, lambda: ts(T.k0[:], T.iob[:], 1.0 / 256, 4.0, ALU.mult, ALU.add), ["iob"], ["k0"])
+    V(8, lambda: ts(T.kb[:, 0:8 * 264:264], T.iob[:, 0:8], 0.0, 16.0, ALU.mult, ALU.add), ["iob"], ["kbi"])
     V(8, lambda: g.vector.memset(T.rb[:, 0:8 * 264:264], -BIG), [], ["rbi"])
     V(1, lambda: g.vector.memset(T.rd[:, 0:1], 0.0), [], ["rd0"])
-    V(16, lambda: g.vector.memset(T.kc[:], 0.0), [], ["kc"])
 
     def W(name, b):
         return (T[name + "q"][:, 128 * b:128 * b + 128], T[name + "p"][:, 128 * b:128 * b + 128])
@@ -184,14 +184,14 @@ def rank_program(g, core, T, topo):
     quant(T.q0[:], T.p0[:], T.xin[:], 256, ["xin"], ["q0"])
     quant(T.u0[:], T.s0[:], T.uin[:], 128, ["uin"], ["u0"])
 
-    def unpack(q, p, to, at, how, scale):
+    def halves(q, p):
         for b in B4:
-            mm((at, b), W("eh", b), (T[q][:], T[p][:]), 256, True, True, ["ehq", q])
-        for b in B4:
-            i, bn = bank((at, b))
-            copy(how[b], T[to][:, 256 * b:256 * b + 256], i, 256, [], ["%s%d" % (to, b), bn], scale)
+            mm(("pr", b), W("eh", b), (T[q][:], T[p][:]), 256, True, True, ["ehq%d" % b, q])
+            if ZS[b] == "V":
+                i, bn = bank(("pr", b))
+                copy(TS[b], T.tp[:, 256 * b:256 * b + 256], i, 256, [], ["tp%d" % b, bn])
 
-    unpack("q0", "p0", "tp", "pr", TS, 0.015625)
+    halves("q0", "p0")
     for r, h in enumerate(STEP):
         qn, un, q2, p2, u2, s2 = "q%d" % r, "u%d" % r, "q%d" % (r + 1), "p%d" % (r + 1), "u%d" % (r + 1), "s%d" % (r + 1)
         Q, U = (T[qn][:], T["p%d" % r][:]), (T[un][:], T["s%d" % r][:])
@@ -208,26 +208,29 @@ def rank_program(g, core, T, topo):
             op("N", lat, None, [sent], writes, sem=arr, inc=len(moves) * ne)
 
         mm(("pd", 0), U, Q, 256, True, True, [qn, un])
-        mm(("pd", 1), U, Q, 256, True, True, [qn, un])
         for b in B4:
-            at = ("pd", 2 + b % 2) if r == 0 else ("pr", b)
-            mm(at, W("eh", b), U, 128, True, True, ["ehq", un])
+            at = ("pd", 2 + b % 2)
+            mm(at, W("eh", b), U, 128, True, True, ["ehq%d" % b, un])
             i, bn = bank(at, 128)
-            copy("A", T.du[:, 128 * b:128 * b + 128], i, 128, [], ["du%d" % b, bn], 0.015625)
-        for b in B4:
-            mm(("pr", b), W("eh", b), Q, 256, True, False, ["ehq", qn])
+            copy("A", T.du[:, 128 * b:128 * b + 128], i, 128, [], ["du%d" % b, bn])
+        mm(("pd", 1), U, Q, 256, True, True, [qn, un])
         V(256, lambda: g.vector.transpose(T.st[:], T.pd[:, 0:256]), [], ["st", "PD0"])
         V(256, lambda: scan(T.rd[:, 1:257], T.seg[:], T.st[:], 0.0, ALU.min, ALU.max), ["seg0", "st"], ["rd"])
         V(256, lambda: tt(T.qd[:], T.rd[:, 0:256], T.st[:], ALU.is_ge), ["rd", "rd0", "st"], ["qd"], 2.0)
-        V(256, lambda: scan(T.cd[:], T.qd[:], T.qd[:], 0.0, ALU.mult, ALU.add), ["qd"], ["cd"], 0.5)
-        V(16, lambda: ts(T.kc[:, 0:16], T.cd[:, 15:256:16], 15.0, None, ALU.min), ["cd"], ["kc"])
-        V(32, lambda: g.vector.transpose(T.kt[:], T.kc[:]), ["kc"], ["kt"])
-        GA(64, lambda: tc(T.kd[:], T.kt[:, 0:32].indirect(T.dupl[:, 0:4])), ["kt", "dupl"], ["kd"])
-        V(64, lambda: g.vector.transpose(T.ko[:], T.kd[:]), ["kd"], ["ko"])
-        GA(16, lambda: ts(T.offd[:], T.ko[:, 0:64].indirect(T.seld[:, 0:1]), -1.0, T.base[:], ALU.mult, ALU.add), ["ko", "seld", "base"], ["offd"])
+        V(256, lambda: scan(T.cd[:, 0:256], T.qd[:], T.qd[:], 0.0, ALU.mult, ALU.subtract), ["qd"], ["cd"], 0.5)
+        for k in (0, 1):
+            V(32, lambda k=k: g.vector.transpose(T.kt[:, 32 * k:32 * k + 32], T.cd[:, 15:512:16]), ["cd", "cd0"], ["kt%d" % k])
+        V(32, lambda: g.vector.transpose(T.cd[:, 512:544], T.kt[:, 16:48]), ["kt0", "kt1"], ["ko"])
+        GA(16, lambda: ts(T.offd[:], T.cd[:, 0:544].indirect(T.seld[:, 0:1]), -15.0, T.base[:], ALU.max, ALU.add), ["cd", "cd0", "ko", "seld", "base"], ["offd"])
         for b in B4:
-            GA(256, lambda b=b: tt(T.zt[:, b:1024:4], T.du[:, 128 * b:128 * b + 128].indirect(T.offd[:, 0:16]), T.tp[:, 256 * b:256 * b + 256], ALU.add),
-               ["du%d" % b, "offd", "tp%d" % b], ["zt%d" % b])
+            o, i, c = T.zt[:, b:1024:4], T.du[:, 128 * b:128 * b + 128].indirect(T.offd[:, 0:16]), slice(256 * b, 256 * b + 256)
+            if ZS[b] == "V":
+                GA(256, lambda o=o, i=i, c=c: tt(o, i, T.tp[:, c], ALU.add), ["du%d" % b, "offd", "tp%d" % b], ["zt%d" % b])
+            else:
+                AG(256, lambda i=i, c=c: act(T.ag[:, c], i, ACTF.Copy), ["du%d" % b, "offd"], ["ag%d" % b])
+                t, bn = bank(("pr", b))
+                V(256, lambda o=o, c=c, t=t: tt(o, T.ag[:, c], t, ALU.add), ["ag%d" % b], ["zt%d" % b, bn])
+            mm(("pr", b), W("ef", b), Q, 256, True, False, ["efq%d" % b, qn])
         quant(Z[0], Z[1], T.zt[:], 256, ["zt%d" % b for b in B4], ["zq%d" % r])
         for b in B4:
             mm(("pr", b), W("w", b), Z, 256, False, True, ["wq", "wp", "zq%d" % r])
@@ -237,56 +240,46 @@ def rank_program(g, core, T, topo):
         quant(T[q2][:], T[p2][:], T.xt[:], 256, ["xt%d" % b for b in B4], [q2])
         send(1.0, 3.0, [(T["xl%d" % r][:].bitcast(dt.uint8), T[q2][:].bitcast(dt.uint8)), (T["xs%d" % r][:], T[p2][:])],
              [q2], ["xl%d" % r], "arr%d" % r, "sent%d" % r)
-        for k in range(8):
-            o, kk = 264 * k, slice(k, k + 1)
-            run, v, w = T.rb[:, o + 1:o + 257], T.rb[:, o + 256:o + 257], T.rb[:, o - 8:o - 7]
-            if k == 0:
-                V(256, lambda run=run: scan(run, T.top[:], T.pd[:, 0:256], -2.0 * BIG, ALU.min, ALU.max), ["top"], ["rb0", "PD0"])
-                A(256, lambda run=run, v=v: act(T.junk[:], run, ACTF.Sign, bias=v, scale=-1.0, accum_out=T.n0[:]), ["rb0"], ["junk", "n0"], 0.1)
-                A(1, lambda: act(T.nb[:, 0:1], T.n0[:], ACTF.Identity, bias=-256.0, scale=2.0), ["n0"], ["nb0"])
-                continue
-            dk, ok = "db%d" % (k % 2), "db%d" % ((k - 1) % 2)
-            out, old, shifted = T[dk][:], T[ok][:], T.rb[:, o - 264:o - 8]
-            if k == 1:
-                V(256, lambda out=out, x=shifted: scan(out, x, T.pd[:, 0:256], -2.0 * BIG, ALU.max, ALU.min), ["rb0", "rbi"], [dk, "PD0"])
-            else:
-                V(256, lambda out=out, x=shifted, old=old: scan(out, x, old, -2.0 * BIG, ALU.max, ALU.min), ["rb%d" % (k - 1), "rbi", ok], [dk])
-            V(256, lambda out=out, run=run: scan(run, out, out, -2.0 * BIG, ALU.max, ALU.max), [dk, "rbi"], ["rb%d" % k])
-            e, c, f = [T[x][:, 256 * k:256 * k + 256] for x in ("neb", "cb", "sgb")]
-            if k in ON_SCALAR:
-                A(256, lambda f=f, v=v, kk=kk: act(f, T.pd[:, 512:768], ACTF.Sign, bias=v, scale=-1.0, accum_out=T.less[:, kk]),
-                  ["rb%d" % k], ["sgb%d" % k, "less%d" % k, "PD1"], 0.08)
-                A(256, lambda f=f, e=e, kk=kk: act(e, f, ACTF.Abs, accum_out=T.more[:, kk]), ["sgb%d" % k], ["neb%d" % k, "more%d" % k], 0.08)
-                A(1, lambda k=k, kk=kk: act(T.part[:, kk], T.less[:, kk], ACTF.Identity, bias=k + 0.5, scale=0.5), ["less%d" % k], ["part%d" % k])
-                A(1, lambda kk=kk: act(T.held[:, kk], T.more[:, kk], ACTF.Identity, bias=T.part[:, kk], scale=-0.5),
-                  ["more%d" % k, "part%d" % k], ["held%d" % k])
-                first, half, need = 0.0, T.held[:, kk], []
-                if k < 7 and k + 1 not in ON_SCALAR:
-                    A(1, lambda kk=kk: act(T.jm[:, kk], T.held[:, kk], ACTF.Identity, bias=0.5), ["held%d" % k], ["jm%d" % k])
-            else:
-                V(256, lambda e=e, v=v: ts(e, T.pd[:, 0:256], v, None, ALU.not_equal), ["rb%d" % k], ["neb%d" % k, "PD0"])
-                V(1, lambda v=v, w=w, k=k, kk=kk: ts(T.jn[:, kk], v, w, T.jm[:, k - 1:k], ALU.is_equal, ALU.mult),
-                  ["rb%d" % k, "rb%d" % (k - 1), "jm%d" % (k - 1)], ["jn%d" % k])
-                if k < 7 and k + 1 not in ON_SCALAR:
-                    A(1, lambda kk=kk: act(T.jm[:, kk], T.jn[:, kk], ACTF.Identity, bias=1.0), ["jn%d" % k], ["jm%d" % k])
-                first, half, need = T.jn[:, kk], 0.5, ["jn%d" % k]
-            V(256, lambda e=e, c=c, first=first: scan(c, e, T.ones[:], first, ALU.add, ALU.subtract), ["neb%d" % k, "ones"] + need, ["cb%d" % k], 0.5)
-            A(256, lambda c=c, kk=kk, half=half: act(T.junk[:], c, ACTF.Sign, bias=half, accum_out=T.nb[:, kk]),
-              ["cb%d" % k] + ([] if need else ["held%d" % k]), ["junk", "nb%d" % k], 0.1)
-        NB = ["nb%d" % k for k in range(8)]
-        for q in B4:
-            copy("VA"[q % 2], T.nb[32 * q:32 * q + 32, 8:16], T.nb[32 * ((q + 1) % 4):32 * ((q + 1) % 4) + 32, 0:8], 8, NB, ["nx%d" % q])
-        NX = NB + ["nx%d" % q for q in B4]
-        copy("V", T.nb[0:64, 16:32], T.nb[64:128, 0:16], 16, NX, ["ny0"])
-        copy("A", T.nb[64:128, 16:32], T.nb[0:64, 0:16], 16, NX, ["ny1"])
-        V(32, lambda: g.vector.transpose(T.nt[:], T.nb[:]), NX + ["ny0", "ny1"], ["nt"])
-        GA(64, lambda: tc(T.nd[:], T.nt[:, 0:32].indirect(T.dupl[:, 0:4])), ["nt", "dupl"], ["nd"])
-        V(64, lambda: g.vector.transpose(T.ngo[:], T.nd[:]), ["nd"], ["ngo"])
-        GA(16, lambda: ts(T.offn[:], T.ngo[:, 0:64].indirect(T.seln[:, 0:1]), 0.5, 128.0, ALU.mult, ALU.add), ["ngo", "seln"], ["offn"])
-        send(0.5, 1.5, [(T["lo%d" % r][:], T.offn[:, 0:8])], ["offn"], ["lo%d" % r], "lst%d" % r, "lsent%d" % r)
-        unpack("xl%d" % r, "xs%d" % r, "tr", "pr", RS, 0.03125)
         if r < 2:
-            unpack(q2, p2, "tp", "pd", TS, 0.015625)
+            halves(q2, p2)
+        for k in range(8):
+            o = 264 * k
+            run, v = T.rb[:, o + 1:o + 257], T.rb[:, o + 256:o + 257]
+            cap, names = (T.top[:], ["top"]) if k == 0 else (T.rb[:, o - 264:o - 8], ["rb%d" % (k - 1), "rbi"])
+            V(256, lambda run=run, cap=cap: scan(run, T.pd[:, 0:256], cap, -2.0 * BIG, ALU.max, ALU.min), names, ["rb%d" % k, "PD0"])
+            if k % 2:
+                j = k // 2
+                f = T.sg[:, 256 * j:256 * j + 256] if j < 3 else T.ki[:, 1:512:2]
+                A(256, lambda f=f, v=v: act(f, T.pd[:, 512:768], ACTF.Sign, bias=v, scale=-1.0), ["rb%d" % k], ["sg%d" % j, "PD1"])
+                if j < 3:
+                    o2, i2 = [T.k1[:], T.k2[:], T.ki[:, 0:512:2]][j], T["k%d" % j][:]
+                    V(128, lambda o2=o2, i2=i2, f=f: scan(o2, f, i2, 1.0, ALU.min, ALU.add), ["sg%d" % j, "k%d" % j], ["k%d" % (j + 1)])
+        V(256, lambda: scan(T.kk[:], T.odd[:], T.ki[:], 0.0, ALU.mult, ALU.add), ["odd0", "odd1", "k3", "sg3"], ["kk"])
+        key = T.kk[:, 1:512:2]
+        for k in range(8):
+            o = 264 * k
+            if k == 0:
+                V(128, lambda: scan(T.kb[:, 1:257], key, key, 16.0, ALU.min, ALU.min), ["kk"], ["kb0"])
+            else:
+                V(128, lambda o=o: scan(T.kb[:, o + 1:o + 257], key, T.kb[:, o - 264:o - 8], 16.0, ALU.min, ALU.max), ["kk", "kbi", "kb%d" % (k - 1)], ["kb%d" % k])
+        KB = ["kb%d" % k for k in range(8)]
+        V(8, lambda: ts(T.fl[:], T.kb[:, 256:8 * 264:264], -0.498, None, ALU.add), KB, ["fl"])
+        for k, (o, i, c) in enumerate([((0, 128), (0, 128), 0), ((0, 64), (64, 128), 8), ((64, 128), (0, 64), 8)]):
+            V(8, lambda o=o, i=i, c=c: tt(T.nb[o[0]:o[1], c:c + 8], T.kb[i[0]:i[1], 256:8 * 264:264], T.fl[i[0]:i[1], :], ALU.subtract), KB + ["fl"], ["nb%d" % k])
+        NB = ["nb%d" % k for k in range(3)]
+        for q in B4:
+            copy(QS[q], T.nb[32 * q:32 * q + 32, 16:32], T.nb[32 * ((q + 1) % 4):32 * ((q + 1) % 4) + 32, 0:16], 16, NB, ["nx%d" % q])
+        NX = NB + ["nx%d" % q for q in B4]
+        for k in (0, 1):
+            V(32, lambda k=k: g.vector.transpose(T.nt[:, 32 * k:32 * k + 32], T.nb[:, 0:32]), NX, ["nt%d" % k])
+        V(32, lambda: g.vector.transpose(T.nb[:, 32:64], T.nt[:, 16:48]), ["nt0", "nt1"], ["no"])
+        GA(16, lambda: ts(T.offn[:], T.nb[:, 0:64].indirect(T.seln[:, 0:1]), 256.0, None, ALU.mult), NX + ["no", "seln"], ["offn"])
+        send(0.5, 1.5, [(T["lo%d" % r][:], T.offn[:, 0:8])], ["offn"], ["lo%d" % r], "lst%d" % r, "lsent%d" % r)
+        for b in B4:
+            at = ("pr", b) if ZS[b] == "V" or r == 2 else ("pd", 2 + b % 2)
+            mm(at, W("ef", b), (T["xl%d" % r][:], T["xs%d" % r][:]), 256, True, True, ["efq%d" % b, "xl%d" % r])
+            i, bn = bank(at)
+            copy(RS[b], T.tr[:, 256 * b:256 * b + 256], i, 256, [], ["tr%d" % b, bn], 0.03125)
         for b in B4:
             o, i = T.vt[:, b:512:4], T.tr[:, 256 * b:256 * b + 256].indirect(T["lo%d" % r][:, 0:8])
             if VS[b] == "A":
@@ -313,7 +306,7 @@ def rank_program(g, core, T, topo):
 
 
 TRIES, FOUND = 700, {}
-ASSUMED = [(1.0, 0.07, 0.0), (0.8, 0.07, 0.0), (1.0, 0.2, 0.0), (1.2, 0.07, 1.0), (0.8, 0.07, 2.0), (1.0, 0.03, 0.0)]
+ASSUMED = [(1.0, 0.07, 0.0), (0.8, 0.07, 0.0), (1.0, 0.2, 0.0), (1.2, 0.07, 1.0), (0.8, 0.15, -1.0), (0.8, 0.2, 0.0)]
 
 
 def find_order(ops):

@@ -4,13 +4,16 @@ ALU = AluOpType
 ACTF = ActivationFunctionType
 STEP = [1, 2, 4]
 BIG = 1.0e29
+H = 2
+NK = 6
+NE = "VVVVVVAV"
 ZS = "AAVV"
 TS, XS, RS, VS, QS = "AAAA", "AAAV", "AAVV", "AAVV", "VAVA"
 
 SCRATCH = {
     "xin": ("sbuf", [128, 1024], "bfloat16"), "uin": ("sbuf", [128, 512], "bfloat16"), "vin": ("sbuf", [128, 512], "bfloat16"),
     "full": ("sbuf", [128, 516], "bfloat16"), "ef": ("sbuf", [128, 516], "bfloat16"), "eh": ("sbuf", [128, 516], "bfloat16"),
-    "iob": ("sbuf", [128, 256], "bfloat16"), "k0": ("sbuf", [128, 256], "float16"), "odd": ("sbuf", [128, 512], "bfloat16"),
+    "iob": ("sbuf", [128, 256], "bfloat16"), "k0": ("sbuf", [128, 256], "float16"), "ones": ("sbuf", [128, 256], "bfloat16"),
     "seg": ("sbuf", [128, 256], "float32"), "top": ("sbuf", [128, 256], "float32"),
     "ib": ("sbuf", [128, 16], "int32"), "fb": ("sbuf", [128, 8], "float32"), "iw": ("sbuf", [128, 8], "int32"), "base": ("sbuf", [128, 1], "float32"),
     "seld": ("sbuf", [128, 2], "uint16"), "seln": ("sbuf", [128, 2], "uint16"),
@@ -18,9 +21,10 @@ SCRATCH = {
     "qd": ("sbuf", [128, 256], "bfloat16"), "cd": ("sbuf", [128, 544], "bfloat16"), "kt": ("sbuf", [128, 64], "bfloat16"),
     "offd": ("sbuf", [128, 16], "uint16"), "offn": ("sbuf", [128, 16], "uint16"),
     "rb": ("sbuf", [128, 8 * 264], "float32"), "kb": ("sbuf", [128, 8 * 264], "float16"),
-    "sg": ("sbuf", [128, 768], "bfloat16"), "k1": ("sbuf", [128, 256], "float16"), "k2": ("sbuf", [128, 256], "float16"),
-    "ki": ("sbuf", [128, 512], "float16"), "kk": ("sbuf", [128, 512], "float16"), "fl": ("sbuf", [128, 8], "int32"),
-    "nb": ("sbuf", [128, 64], "bfloat16"), "nt": ("sbuf", [128, 64], "bfloat16"),
+    "sg": ("sbuf", [128, 2048], "bfloat16"), "ne": ("sbuf", [128, 2048], "bfloat16"), "cn": ("sbuf", [128, 2048], "bfloat16"),
+    "k1": ("sbuf", [128, 256], "float16"), "k2": ("sbuf", [128, 256], "float16"), "k3": ("sbuf", [128, 256], "float16"),
+    "fl": ("sbuf", [128, 8], "int32"), "ac": ("sbuf", [128, 8], "float32"), "junk": ("sbuf", [128, 64], "bfloat16"),
+    "nb": ("sbuf", [128, 64], "float32"), "nt": ("sbuf", [128, 64], "float32"),
     "du": ("sbuf", [128, 512], "bfloat16"), "tp": ("sbuf", [128, 1024], "bfloat16"), "tr": ("sbuf", [128, 1024], "bfloat16"),
     "ag": ("sbuf", [128, 1024], "bfloat16"),
     "zt": ("sbuf", [128, 1024], "bfloat16"), "xt": ("sbuf", [128, 1024], "bfloat16"), "vt": ("sbuf", [128, 512], "bfloat16"),
@@ -46,10 +50,10 @@ for _r in range(3):
     _pair("xl%d" % _r, "xs%d" % _r, 256)
     SCRATCH["lo%d" % _r] = ("sbuf", [128, 8], "uint16")
 
-SEMAPHORES = ["sv", "sa", "sp", "sg"] + ["%s%d" % (n, r) for n in ("arr", "sent", "lst", "lsent") for r in range(3)] + ["d%d" % k for k in range(24)]
+SEMAPHORES = (["sv", "sa", "sp", "sg"] + ["%s%d" % (n, r) for n in ("arra", "arrb", "senta", "sentb", "lst", "lsent") for r in range(3)]
+              + ["d%d" % k for k in range(24)])
 
 CYC = 0.00083 * 1.25
-WAKE = 0.07
 
 
 def rank_program(g, core, T, topo):
@@ -94,8 +98,8 @@ def rank_program(g, core, T, topo):
     def AG(n, fn, reads, writes):
         op("A", 0.065 + n * 1.5 * CYC, fn, reads, writes)
 
-    def bank(b, n=256):
-        return T[b[0]][:, 512 * b[1]:512 * b[1] + n], b[0].upper() + "%d" % b[1]
+    def bank(b, n=256, c=0):
+        return T[b[0]][:, 512 * b[1] + c:512 * b[1] + c + n], b[0].upper() + "%d" % b[1]
 
     def mm(b, lhs, rhs, n, start, stop, reads):
         out, name = bank(b, n)
@@ -167,11 +171,12 @@ def rank_program(g, core, T, topo):
     V(1, lambda: ts(fcol(3), col(9), 16.0, fcol(2), ALU.mult, ALU.add), ["ib9", "fb2"], ["fb3"])
     V(1, lambda: ts(fcol(4), col(10), 4.0, fcol(3), ALU.mult, ALU.add), ["ib10", "fb3"], ["fb4"])
     V(1, lambda: ts(T.seln[:, 0:1], col(6), 32.0, fcol(4), ALU.mult, ALU.add), ["ib6", "fb4"], ["seln"])
+    V(1, lambda: ts(fcol(5), col(5), float(NK), 128.0, ALU.is_ge, ALU.mult), ["ib5"], ["fb5"])
+    V(1, lambda: ts(fcol(6), fcol(5), -255.5 / 128, 256.0, ALU.mult, ALU.add), ["fb5"], ["fb6"])
     A(256, lambda: act(T.top[:], T.iob[:], ACTF.Identity, bias=BIG, scale=0.0), ["iob"], ["top"])
     A(256, lambda: act(T.seg[:], T.iob[:], ACTF.Identity, bias=BIG, scale=0.0), ["iob"], ["seg0"])
     A(16, lambda: act(T.seg[:, 0:256:16], T.iob[:, 0:16], ACTF.Identity, bias=-BIG, scale=0.0), ["iob", "seg0"], ["seg0"])
-    A(256, lambda: act(T.odd[:, 0:512:2], T.iob[:], ACTF.Identity, bias=0.0, scale=0.0), ["iob"], ["odd0"])
-    A(256, lambda: act(T.odd[:, 1:512:2], T.iob[:], ACTF.Identity, bias=1.0, scale=0.0), ["iob"], ["odd1"])
+    A(256, lambda: act(T.ones[:], T.iob[:], ACTF.Identity, bias=1.0, scale=0.0), ["iob"], ["ones"])
     A(256, lambda: act(T.cd[:, 256:512], T.iob[:], ACTF.Copy), ["iob"], ["cd0"])
     V(128, lambda: ts(T.k0[:], T.iob[:], 1.0 / 256, 4.0, ALU.mult, ALU.add), ["iob"], ["k0"])
     V(8, lambda: ts(T.kb[:, 0:8 * 264:264], T.iob[:, 0:8], 0.0, 16.0, ALU.mult, ALU.add), ["iob"], ["kbi"])
@@ -181,21 +186,25 @@ def rank_program(g, core, T, topo):
     def W(name, b):
         return (T[name + "q"][:, 128 * b:128 * b + 128], T[name + "p"][:, 128 * b:128 * b + 128])
 
-    quant(T.q0[:], T.p0[:], T.xin[:], 256, ["xin"], ["q0"])
+    RUNS = [(c, 256 // H, "ab"[c * H // 256]) for c in range(0, 256, 256 // H)]
+    quant(T.q0[:], T.p0[:], T.xin[:], 256, ["xin"], ["q0" + x for _, _, x in RUNS])
     quant(T.u0[:], T.s0[:], T.uin[:], 128, ["uin"], ["u0"])
 
     def halves(q, p):
         for b in B4:
-            mm(("pr", b), W("eh", b), (T[q][:], T[p][:]), 256, True, True, ["ehq%d" % b, q])
+            mm(("pr", b), W("eh", b), (T[q][:], T[p][:]), 256, True, True, ["ehq%d" % b] + [q + x for _, _, x in RUNS])
             if ZS[b] == "V":
                 i, bn = bank(("pr", b))
                 copy(TS[b], T.tp[:, 256 * b:256 * b + 256], i, 256, [], ["tp%d" % b, bn])
 
+    early = [("pr", b) for b in B4 if ZS[b] == "V"] + [("pd", 2), ("pd", 3)]
+    late = early[4:] + [("pr", b) for b in B4 if ZS[b] != "V"]
+    SUMS = [[("pr", b) for b in B4]] if H == 1 else [early[:4], (late + early)[:4]]
+
     halves("q0", "p0")
     for r, h in enumerate(STEP):
-        qn, un, q2, p2, u2, s2 = "q%d" % r, "u%d" % r, "q%d" % (r + 1), "p%d" % (r + 1), "u%d" % (r + 1), "s%d" % (r + 1)
-        Q, U = (T[qn][:], T["p%d" % r][:]), (T[un][:], T["s%d" % r][:])
-        Z = (T["zq%d" % r][:], T["zp%d" % r][:])
+        qn, pn, un, q2, p2, u2, s2 = "q%d" % r, "p%d" % r, "u%d" % r, "q%d" % (r + 1), "p%d" % (r + 1), "u%d" % (r + 1), "s%d" % (r + 1)
+        Q, U, QN = (T[qn][:], T[pn][:]), (T[un][:], T["s%d" % r][:]), [qn + x for _, _, x in RUNS]
         dst = T.cores[(rank + h) % len(T.cores)]
         rid, pid, _ = topo.addr(dst)
         m, ne = topo.mask(core, dst), len(topo.engines(core, dst))
@@ -207,14 +216,14 @@ def rank_program(g, core, T, topo):
             op("G", cost, go, reads, [sent], sem=sent, inc=len(moves) * ne)
             op("N", lat, None, [sent], writes, sem=arr, inc=len(moves) * ne)
 
-        mm(("pd", 0), U, Q, 256, True, True, [qn, un])
+        mm(("pd", 0), U, Q, 256, True, True, QN + [un])
         for b in B4:
             at = ("pd", 2 + b % 2)
             mm(at, W("eh", b), U, 128, True, True, ["ehq%d" % b, un])
             i, bn = bank(at, 128)
             copy("A", T.du[:, 128 * b:128 * b + 128], i, 128, [], ["du%d" % b, bn])
-        mm(("pd", 1), U, Q, 256, True, True, [qn, un])
-        V(256, lambda: g.vector.transpose(T.st[:], T.pd[:, 0:256]), [], ["st", "PD0"])
+        mm(("pd", 1), U, Q, 256, True, True, QN + [un])
+        V(256, lambda: g.vector.transpose(T.st[:], T.pd[:, 0:256]), ["PD0"], ["st"])
         V(256, lambda: scan(T.rd[:, 1:257], T.seg[:], T.st[:], 0.0, ALU.min, ALU.max), ["seg0", "st"], ["rd"])
         V(256, lambda: tt(T.qd[:], T.rd[:, 0:256], T.st[:], ALU.is_ge), ["rd", "rd0", "st"], ["qd"], 2.0)
         V(256, lambda: scan(T.cd[:, 0:256], T.qd[:], T.qd[:], 0.0, ALU.mult, ALU.subtract), ["qd"], ["cd"], 0.5)
@@ -222,78 +231,96 @@ def rank_program(g, core, T, topo):
             V(32, lambda k=k: g.vector.transpose(T.kt[:, 32 * k:32 * k + 32], T.cd[:, 15:512:16]), ["cd", "cd0"], ["kt%d" % k])
         V(32, lambda: g.vector.transpose(T.cd[:, 512:544], T.kt[:, 16:48]), ["kt0", "kt1"], ["ko"])
         GA(16, lambda: ts(T.offd[:], T.cd[:, 0:544].indirect(T.seld[:, 0:1]), -15.0, T.base[:], ALU.max, ALU.add), ["cd", "cd0", "ko", "seld", "base"], ["offd"])
-        for b in B4:
-            o, i, c = T.zt[:, b:1024:4], T.du[:, 128 * b:128 * b + 128].indirect(T.offd[:, 0:16]), slice(256 * b, 256 * b + 256)
-            if ZS[b] == "V":
-                GA(256, lambda o=o, i=i, c=c: tt(o, i, T.tp[:, c], ALU.add), ["du%d" % b, "offd", "tp%d" % b], ["zt%d" % b])
-            else:
-                AG(256, lambda i=i, c=c: act(T.ag[:, c], i, ACTF.Copy), ["du%d" % b, "offd"], ["ag%d" % b])
-                t, bn = bank(("pr", b))
-                V(256, lambda o=o, c=c, t=t: tt(o, T.ag[:, c], t, ALU.add), ["ag%d" % b], ["zt%d" % b, bn])
-            mm(("pr", b), W("ef", b), Q, 256, True, False, ["efq%d" % b, qn])
-        quant(Z[0], Z[1], T.zt[:], 256, ["zt%d" % b for b in B4], ["zq%d" % r])
-        for b in B4:
-            mm(("pr", b), W("w", b), Z, 256, False, True, ["wq", "wp", "zq%d" % r])
-        for b in B4:
-            i, bn = bank(("pr", b))
-            copy(XS[b], T.xt[:, b:1024:4], i, 256, [], ["xt%d" % b, bn], 0.03125)
-        quant(T[q2][:], T[p2][:], T.xt[:], 256, ["xt%d" % b for b in B4], [q2])
-        send(1.0, 3.0, [(T["xl%d" % r][:].bitcast(dt.uint8), T[q2][:].bitcast(dt.uint8)), (T["xs%d" % r][:], T[p2][:])],
-             [q2], ["xl%d" % r], "arr%d" % r, "sent%d" % r)
+        for (c, n, x), sums in zip(RUNS, SUMS):
+            for b in B4:
+                o, i = T.zt[:, 4 * c + b:4 * (c + n):4], T.du[:, 128 * b:128 * b + 128].indirect(T.offd[:, c // 16:(c + n) // 16])
+                at = slice(256 * b + c, 256 * b + c + n)
+                if ZS[b] == "V":
+                    GA(n, lambda o=o, i=i, at=at: tt(o, i, T.tp[:, at], ALU.add), ["du%d" % b, "offd", "tp%d" % b], ["zt%d" % b + x])
+                else:
+                    AG(n, lambda i=i, at=at: act(T.ag[:, at], i, ACTF.Copy), ["du%d" % b, "offd"], ["ag%d" % b + x])
+                    t, bn = bank(("pr", b), n, c)
+                    V(n, lambda o=o, at=at, t=t: tt(o, T.ag[:, at], t, ALU.add), ["ag%d" % b + x, bn], ["zt%d" % b + x])
+            Z = (T["zq%d" % r][:, c:c + n], T["zp%d" % r][:, c:c + n])
+            quant(Z[0], Z[1], T.zt[:, 4 * c:4 * (c + n)], n, ["zt%d" % b + x for b in B4], ["zq%d" % r + x])
+            for b in B4:
+                mm(sums[b], W("ef", b), (T[qn][:, c:c + n], T[pn][:, c:c + n]), n, True, False, ["efq%d" % b, qn + x])
+                mm(sums[b], W("w", b), Z, n, False, True, ["wq", "wp", "zq%d" % r + x])
+                i, bn = bank(sums[b], n)
+                copy(XS[b], T.xt[:, 4 * c + b:4 * (c + n):4], i, n, [], ["xt%d" % b + x, bn], 0.03125)
+            quant(T[q2][:, c:c + n], T[p2][:, c:c + n], T.xt[:, 4 * c:4 * (c + n)], n, ["xt%d" % b + x for b in B4], [q2 + x])
+            send(1.0, 1.0 + 2.0 / H, [(T["xl%d" % r][:, c:c + n].bitcast(dt.uint8), T[q2][:, c:c + n].bitcast(dt.uint8)),
+                                      (T["xs%d" % r][:, c:c + n], T[p2][:, c:c + n])],
+                 [q2 + x], ["xl%d" % r + x], "arr%s%d" % (x, r), "sent%s%d" % (x, r))
         if r < 2:
             halves(q2, p2)
+        else:
+            mm(("pd", 2), (T.vcq[:], T.vcp[:]), (T.q3[:], T.p3[:]), 256, True, True, ["vcq"] + ["q3" + x for _, _, x in RUNS])
+            copy("A", T.ysb[:], bank(("pd", 2))[0], 256, [], ["ysb", "PD2"])
         for k in range(8):
-            o = 264 * k
+            o, kk = 264 * k, slice(k, k + 1)
             run, v = T.rb[:, o + 1:o + 257], T.rb[:, o + 256:o + 257]
             cap, names = (T.top[:], ["top"]) if k == 0 else (T.rb[:, o - 264:o - 8], ["rb%d" % (k - 1), "rbi"])
-            V(256, lambda run=run, cap=cap: scan(run, T.pd[:, 0:256], cap, -2.0 * BIG, ALU.max, ALU.min), names, ["rb%d" % k, "PD0"])
-            if k % 2:
+            V(256, lambda run=run, cap=cap: scan(run, T.pd[:, 0:256], cap, -2.0 * BIG, ALU.max, ALU.min), names + ["PD0"], ["rb%d" % k])
+            f, e, cn = [T[x][:, 256 * k:256 * k + 256] for x in ("sg", "ne", "cn")]
+            if k % 2 and k < NK or k >= NK and NE[k] == "A":
+                A(256, lambda f=f, v=v: act(f, T.pd[:, 512:768], ACTF.Sign, bias=v, scale=-1.0), ["rb%d" % k, "PD1"], ["sg%d" % k])
+            if k % 2 and k < NK:
                 j = k // 2
-                f = T.sg[:, 256 * j:256 * j + 256] if j < 3 else T.ki[:, 1:512:2]
-                A(256, lambda f=f, v=v: act(f, T.pd[:, 512:768], ACTF.Sign, bias=v, scale=-1.0), ["rb%d" % k], ["sg%d" % j, "PD1"])
-                if j < 3:
-                    o2, i2 = [T.k1[:], T.k2[:], T.ki[:, 0:512:2]][j], T["k%d" % j][:]
-                    V(128, lambda o2=o2, i2=i2, f=f: scan(o2, f, i2, 1.0, ALU.min, ALU.add), ["sg%d" % j, "k%d" % j], ["k%d" % (j + 1)])
-        V(256, lambda: scan(T.kk[:], T.odd[:], T.ki[:], 0.0, ALU.mult, ALU.add), ["odd0", "odd1", "k3", "sg3"], ["kk"])
-        key = T.kk[:, 1:512:2]
-        for k in range(8):
+                V(128, lambda j=j, f=f: scan(T["k%d" % (j + 1)][:], f, T["k%d" % j][:], 1.0, ALU.min, ALU.add), ["sg%d" % k, "k%d" % j], ["k%d" % (j + 1)])
+            if k < NK:
+                continue
+            if NE[k] == "A":
+                A(256, lambda f=f, e=e: act(e, f, ACTF.Abs), ["sg%d" % k], ["ne%d" % k])
+            else:
+                V(256, lambda e=e, v=v: ts(e, T.pd[:, 0:256], v, None, ALU.not_equal), ["rb%d" % k, "PD0"], ["ne%d" % k])
+            A(8, lambda k=k, v=v, kk=kk: act(T.junk[:, 8 * k:9 * k], T.rb[:, 256:264 * k:264], ACTF.Sign, bias=v, scale=-1.0, accum_out=T.ac[:, kk]),
+              ["rb%d" % j for j in range(k + 1)], ["ac%d" % k], 0.08)
+            V(128, lambda k=k, e=e, cn=cn: scan(cn, e, T.ones[:], k + 0.5, ALU.add, ALU.subtract), ["ne%d" % k, "ones"], ["cn%d" % k])
+            A(256, lambda cn=cn, kk=kk: act(cn, cn, ACTF.Sign, bias=T.ac[:, kk], accum_out=T.nb[:, kk]), ["ac%d" % k], ["cn%d" % k, "nb%d" % k], 0.08)
+        kn = "k%d" % (NK // 2)
+        for k in range(NK):
             o = 264 * k
             if k == 0:
-                V(128, lambda: scan(T.kb[:, 1:257], key, key, 16.0, ALU.min, ALU.min), ["kk"], ["kb0"])
+                V(128, lambda: scan(T.kb[:, 1:257], T[kn][:], T[kn][:], 16.0, ALU.min, ALU.min), [kn], ["kb0"])
             else:
-                V(128, lambda o=o: scan(T.kb[:, o + 1:o + 257], key, T.kb[:, o - 264:o - 8], 16.0, ALU.min, ALU.max), ["kk", "kbi", "kb%d" % (k - 1)], ["kb%d" % k])
-        KB = ["kb%d" % k for k in range(8)]
-        V(8, lambda: ts(T.fl[:], T.kb[:, 256:8 * 264:264], -0.498, None, ALU.add), KB, ["fl"])
-        for k, (o, i, c) in enumerate([((0, 128), (0, 128), 0), ((0, 64), (64, 128), 8), ((64, 128), (0, 64), 8)]):
-            V(8, lambda o=o, i=i, c=c: tt(T.nb[o[0]:o[1], c:c + 8], T.kb[i[0]:i[1], 256:8 * 264:264], T.fl[i[0]:i[1], :], ALU.subtract), KB + ["fl"], ["nb%d" % k])
-        NB = ["nb%d" % k for k in range(3)]
+                V(128, lambda o=o: scan(T.kb[:, o + 1:o + 257], T[kn][:], T.kb[:, o - 264:o - 8], 16.0, ALU.min, ALU.max), [kn, "kbi", "kb%d" % (k - 1)], ["kb%d" % k])
+        KB = ["kb%d" % k for k in range(NK)]
+        V(8, lambda: ts(T.fl[:, 0:NK], T.kb[:, 256:NK * 264:264], -0.498, None, ALU.add), KB, ["fl"])
+        V(8, lambda: tt(T.nb[:, 0:NK], T.kb[:, 256:NK * 264:264], T.fl[:, 0:NK], ALU.subtract), KB + ["fl"], ["nbk"])
+        NB = ["nbk"] + ["nb%d" % k for k in range(NK, 8)]
+        copy("V", T.nb[0:64, 8:16], T.nb[64:128, 0:8], 8, NB, ["nh0"])
+        copy("A", T.nb[64:128, 8:16], T.nb[0:64, 0:8], 8, NB, ["nh1"])
+        NB = NB + ["nh0", "nh1"]
         for q in B4:
             copy(QS[q], T.nb[32 * q:32 * q + 32, 16:32], T.nb[32 * ((q + 1) % 4):32 * ((q + 1) % 4) + 32, 0:16], 16, NB, ["nx%d" % q])
         NX = NB + ["nx%d" % q for q in B4]
         for k in (0, 1):
             V(32, lambda k=k: g.vector.transpose(T.nt[:, 32 * k:32 * k + 32], T.nb[:, 0:32]), NX, ["nt%d" % k])
         V(32, lambda: g.vector.transpose(T.nb[:, 32:64], T.nt[:, 16:48]), ["nt0", "nt1"], ["no"])
-        GA(16, lambda: ts(T.offn[:], T.nb[:, 0:64].indirect(T.seln[:, 0:1]), 256.0, None, ALU.mult), NX + ["no", "seln"], ["offn"])
+        GA(16, lambda: ts(T.offn[:], T.nb[:, 0:64].indirect(T.seln[:, 0:1]), fcol(6), fcol(5), ALU.mult, ALU.add), NX + ["no", "seln", "fb5", "fb6"], ["offn"])
         send(0.5, 1.5, [(T["lo%d" % r][:], T.offn[:, 0:8])], ["offn"], ["lo%d" % r], "lst%d" % r, "lsent%d" % r)
-        for b in B4:
-            at = ("pr", b) if ZS[b] == "V" or r == 2 else ("pd", 2 + b % 2)
-            mm(at, W("ef", b), (T["xl%d" % r][:], T["xs%d" % r][:]), 256, True, True, ["efq%d" % b, "xl%d" % r])
-            i, bn = bank(at)
-            copy(RS[b], T.tr[:, 256 * b:256 * b + 256], i, 256, [], ["tr%d" % b, bn], 0.03125)
+        free = early if r < 2 else [("pr", b) for b in B4]
+        for c, n, x in RUNS:
+            for b in B4:
+                at = free[b % len(free)]
+                mm(at, W("ef", b), (T["xl%d" % r][:, c:c + n], T["xs%d" % r][:, c:c + n]), n, True, True, ["efq%d" % b, "xl%d" % r + x])
+                i, bn = bank(at, n)
+                copy(RS[b], T.tr[:, 256 * b + c:256 * b + c + n], i, n, [], ["tr%d" % b + x, bn], 0.03125)
         for b in B4:
             o, i = T.vt[:, b:512:4], T.tr[:, 256 * b:256 * b + 256].indirect(T["lo%d" % r][:, 0:8])
+            need = ["tr%d" % b + x for _, _, x in RUNS] + ["lo%d" % r]
             if VS[b] == "A":
-                AG(128, lambda o=o, i=i: act(o, i, ACTF.Copy), ["tr%d" % b, "lo%d" % r], ["vt%d" % b])
+                AG(128, lambda o=o, i=i: act(o, i, ACTF.Copy), need, ["vt%d" % b])
             else:
-                GA(128, lambda o=o, i=i: tc(o, i), ["tr%d" % b, "lo%d" % r], ["vt%d" % b])
+                GA(128, lambda o=o, i=i: tc(o, i), need, ["vt%d" % b])
         quant(T[u2][:], T[s2][:], T.vt[:], 128, ["vt%d" % b for b in B4], [u2])
         if r == 0:
             quant(T.vcq[:], T.vcp[:], T.vin[:], 128, ["vin"], ["vcq"])
-    mm(("pd", 2), (T.vcq[:], T.vcp[:]), (T.q3[:], T.p3[:]), 256, True, True, ["vcq", "q3"])
-    copy("A", T.ysb[:], bank(("pd", 2))[0], 256, [], ["ysb", "PD2"])
-    dma("S", T.oc[:], T.q3[:].bitcast(dt.uint8), ["q3"], [])
+    Q3 = ["q3" + x for _, _, x in RUNS]
+    dma("S", T.oc[:], T.q3[:].bitcast(dt.uint8), Q3, [])
     for k in B4:
-        dma("S", T.osc[4 * k:4 * k + 4, :], T.p3[32 * k:32 * k + 4, :], ["q3"], [])
+        dma("S", T.osc[4 * k:4 * k + 4, :], T.p3[32 * k:32 * k + 4, :], Q3, [])
     dma("S", T.y[:], T.ysb[:], ["ysb"], [])
     AG(256, lambda: act(T.opk[:], T.iob[:].indirect(T.offd[:, 0:16]), ACTF.Copy), ["iob", "offd"], ["opk"])
     AG(128, lambda: act(T.opn[:], T.iob[:].indirect(T.offn[:, 0:8]), ACTF.Copy), ["iob", "offn"], ["opn"])
@@ -305,53 +332,56 @@ def rank_program(g, core, T, topo):
     plan_and_emit(g, T, ops, queue, csem)
 
 
-TRIES, FOUND = 700, {}
-ASSUMED = [(1.0, 0.07, 0.0), (0.8, 0.07, 0.0), (1.0, 0.2, 0.0), (1.2, 0.07, 1.0), (0.8, 0.15, -1.0), (0.8, 0.2, 0.0)]
+TRIES, MOVES, FOUND = 600, 60000, {}
+ASSUMED = [(0.8, 0.2, 0.0), (1.0, 0.07, 0.5), (1.2, 0.25, -0.5)]
 
 
 def find_order(ops):
     n = len(ops)
     unit, cost, extra, hard = [o["u"] for o in ops], [o["cost"] for o in ops], [o["extra"] for o in ops], [sorted(o["hard"]) for o in ops]
-    need = [len(o["hard"] | o["order"]) for o in ops]
+    pred = [sorted(o["hard"] | o["order"]) for o in ops]
     succ = [[] for _ in range(n)]
-    for o in ops:
-        for d in o["hard"] | o["order"]:
-            succ[d].append(o["k"])
+    for k in range(n):
+        for d in pred[k]:
+            succ[d].append(k)
+    takes = [[late + cost[k] if unit[k] == "N" else cost[k] * f if unit[k] in "VAP" else cost[k] for k in range(n)] for f, _, late in ASSUMED]
+    wake0, take0 = ASSUMED[0][1], takes[0]
     tail = [0.0] * n
     for k in range(n - 1, -1, -1):
-        tail[k] = cost[k] + extra[k] + max([tail[s] + WAKE for s in succ[k]] + [0.0])
+        tail[k] = take0[k] + extra[k] + max([tail[s] + wake0 for s in succ[k]] + [0.0])
 
     def plan(key):
-        left, free, end, seq = list(need), {u: 0.0 for u in unit}, [0.0] * n, []
+        left, free, end, seq = [len(d) for d in pred], {u: 0.0 for u in unit}, [0.0] * n, []
         ready = {k: 0.0 for k in range(n) if left[k] == 0}
         while ready:
             est = [(max(t, free[unit[k]]), k) for k, t in ready.items()]
             lo = min(est)[0] + 0.06
             t, k = max((e for e in est if e[0] <= lo), key=lambda e: (key[e[1]], -e[1]))
-            free[unit[k]] = t + cost[k]
-            end[k] = t + cost[k] + extra[k]
+            free[unit[k]] = 0.0 if unit[k] == "N" else t + take0[k]
+            end[k] = t + take0[k] + extra[k]
             seq.append(k)
             del ready[k]
             for s in succ[k]:
                 left[s] -= 1
                 if left[s] == 0:
-                    ready[s] = max([end[d] + WAKE for d in hard[s]] + [0.0])
+                    ready[s] = max([end[d] + wake0 for d in hard[s]] + [0.0])
         return seq
 
     def ends(seq):
         total = 0.0
-        for f, wake, late in ASSUMED:
-            free, end = {u: 0.0 for u in unit}, [0.0] * n
+        for (_, wake, _), take in zip(ASSUMED, takes):
+            free, end = {u: 0.0 for u in "VAPGSN"}, [0.0] * n
             for k in seq:
                 u = unit[k]
-                t = 0.0 if u == "N" else free[u]
+                t = free[u]
                 for d in hard[k]:
-                    if end[d] + wake > t:
-                        t = end[d] + wake
-                t += late + cost[k] if u == "N" else cost[k] * f if u in "VAP" else cost[k]
-                free[u] = t
-                end[k] = t + extra[k]
-            total += max(end)
+                    if end[d] > t:
+                        t = end[d]
+                t += take[k]
+                if u != "N":
+                    free[u] = t
+                end[k] = t + extra[k] + wake
+            total += max(end) + 0.0005 * sum(end) / n
         return total
 
     state = [12345]
@@ -370,6 +400,24 @@ def find_order(ops):
         e = ends(seq)
         if e < least:
             best, least, key = seq, e, trial
+    seq, now = list(best), least
+    for i in range(MOVES):
+        a = rnd(n)
+        k = seq[a]
+        step, b, left = (1, -1)[rnd(2)], a, 1 + (0, 0, 1, 2)[rnd(4)]
+        stop = succ[k] if step == 1 else pred[k]
+        while left and 0 <= b + step < n and seq[b + step] not in stop:
+            b += step
+            left -= unit[seq[b]] == unit[k]
+        if left:
+            continue
+        trial = seq[:a] + seq[a + 1:]
+        trial.insert(b, k)
+        e = ends(trial)
+        if e < now + 0.25 * (1.0 - i / MOVES) ** 2 * rnd(1000) / 1000.0:
+            seq, now = trial, e
+            if e < least:
+                best, least = trial, e
     return best
 
 

from concourse.mybir import dt, AluOpType, ActivationFunctionType

ALU = AluOpType
ACTF = ActivationFunctionType
STEP = [1, 2, 4]
BIG = 1.0e29
H = 2
NK = 6
NE = "VVVVVVAV"
ZS = "AAVV"
TS, XS, RS, VS, QS = "AAAA", "AAAV", "AAVV", "AAVV", "VAVA"

SCRATCH = {
    "xin": ("sbuf", [128, 1024], "bfloat16"), "uin": ("sbuf", [128, 512], "bfloat16"), "vin": ("sbuf", [128, 512], "bfloat16"),
    "full": ("sbuf", [128, 516], "bfloat16"), "ef": ("sbuf", [128, 516], "bfloat16"), "eh": ("sbuf", [128, 516], "bfloat16"),
    "iob": ("sbuf", [128, 256], "bfloat16"), "k0": ("sbuf", [128, 256], "float16"), "ones": ("sbuf", [128, 256], "bfloat16"),
    "seg": ("sbuf", [128, 256], "float32"), "top": ("sbuf", [128, 256], "float32"),
    "ib": ("sbuf", [128, 16], "int32"), "fb": ("sbuf", [128, 8], "float32"), "iw": ("sbuf", [128, 8], "int32"), "base": ("sbuf", [128, 1], "float32"),
    "seld": ("sbuf", [128, 2], "uint16"), "seln": ("sbuf", [128, 2], "uint16"),
    "st": ("sbuf", [128, 256], "float32"), "rd": ("sbuf", [128, 264], "float32"),
    "qd": ("sbuf", [128, 256], "bfloat16"), "cd": ("sbuf", [128, 544], "bfloat16"), "kt": ("sbuf", [128, 64], "bfloat16"),
    "offd": ("sbuf", [128, 16], "uint16"), "offn": ("sbuf", [128, 16], "uint16"),
    "rb": ("sbuf", [128, 8 * 264], "float32"), "kb": ("sbuf", [128, 8 * 264], "float16"),
    "sg": ("sbuf", [128, 2048], "bfloat16"), "ne": ("sbuf", [128, 2048], "bfloat16"), "cn": ("sbuf", [128, 2048], "bfloat16"),
    "k1": ("sbuf", [128, 256], "float16"), "k2": ("sbuf", [128, 256], "float16"), "k3": ("sbuf", [128, 256], "float16"),
    "fl": ("sbuf", [128, 8], "int32"), "ac": ("sbuf", [128, 8], "float32"), "junk": ("sbuf", [128, 64], "bfloat16"),
    "nb": ("sbuf", [128, 64], "float32"), "nt": ("sbuf", [128, 64], "float32"),
    "du": ("sbuf", [128, 512], "bfloat16"), "tp": ("sbuf", [128, 1024], "bfloat16"), "tr": ("sbuf", [128, 1024], "bfloat16"),
    "ag": ("sbuf", [128, 1024], "bfloat16"),
    "zt": ("sbuf", [128, 1024], "bfloat16"), "xt": ("sbuf", [128, 1024], "bfloat16"), "vt": ("sbuf", [128, 512], "bfloat16"),
    "opk": ("sbuf", [128, 256], "float32"), "opn": ("sbuf", [128, 128], "float32"), "ysb": ("sbuf", [128, 256], "float32"),
    "pd": ("psum", [128, 2048], "float32"), "pr": ("psum", [128, 2048], "float32"),
}


def _pair(name, plane, n):
    SCRATCH[name] = ("sbuf", [128, n], "float8_e4m3fn_x4")
    SCRATCH[plane] = ("sbuf", [128, n], "uint8")


_pair("wq", "wp", 512)
_pair("ehq", "ehp", 512)
_pair("efq", "efp", 512)
_pair("vcq", "vcp", 128)
for _r in range(4):
    _pair("q%d" % _r, "p%d" % _r, 256)
    _pair("u%d" % _r, "s%d" % _r, 128)
for _r in range(3):
    _pair("zq%d" % _r, "zp%d" % _r, 256)
    _pair("xl%d" % _r, "xs%d" % _r, 256)
    SCRATCH["lo%d" % _r] = ("sbuf", [128, 8], "uint16")

SEMAPHORES = (["sv", "sa", "sp", "sg"] + ["%s%d" % (n, r) for n in ("arra", "arrb", "senta", "sentb", "lst", "lsent") for r in range(3)]
              + ["d%d" % k for k in range(24)])

CYC = 0.00083 * 1.25


def rank_program(g, core, T, topo):
    rank = T.rank_of(core)
    if rank is None:
        return
    ops = []
    last_w, readers = {}, {}
    queue = {"V": g.vector, "A": g.scalar, "P": g.tensor, "G": g, "S": g.sync, "AD": g.scalar}
    csem = {"V": "sv", "A": "sa", "P": "sp", "G": "sg"}
    ndma = [0]

    def op(eng, cost, fn, reads=(), writes=(), sem=None, inc=1, extra=0.0):
        k = len(ops)
        hard, order = set(), set()
        for b in reads:
            if b in last_w:
                hard.add(last_w[b])
        for b in writes:
            for d in ([last_w[b]] if b in last_w else []) + readers.get(b, []):
                if eng == "P" and ops[d]["eng"] == "P" and b[:2] in ("PD", "PR"):
                    order.add(d)
                else:
                    hard.add(d)
        for b in reads:
            readers.setdefault(b, []).append(k)
        for b in writes:
            last_w[b] = k
            readers[b] = []
        ops.append({"k": k, "eng": eng, "u": "A" if eng == "AD" else eng, "cost": cost, "extra": extra, "fn": fn,
                    "hard": hard - {k}, "order": order - {k}, "sem": sem, "inc": inc, "w": list(writes)})

    def V(n, fn, reads, writes, cyc=1.0):
        op("V", max(64, n * cyc) * CYC, fn, reads, writes)

    def GA(n, fn, reads, writes):
        op("V", 0.05 + n * 1.5 * CYC, fn, reads, writes)

    def A(n, fn, reads, writes, fix=0.06):
        op("A", fix + n * CYC, fn, reads, writes)

    def AG(n, fn, reads, writes):
        op("A", 0.065 + n * 1.5 * CYC, fn, reads, writes)

    def bank(b, n=256, c=0):
        return T[b[0]][:, 512 * b[1] + c:512 * b[1] + c + n], b[0].upper() + "%d" % b[1]

    def mm(b, lhs, rhs, n, start, stop, reads):
        out, name = bank(b, n)
        op("P", (n + 16) * CYC, lambda: g.tensor.matmul_mx(out, lhs[0], lhs[1], rhs[0], rhs[1], start, stop), reads, [name])

    def dma(eng, out, in_, reads, writes, lat=2.2):
        s = "d%d" % ndma[0]
        ndma[0] += 1
        op(eng, 0.08, lambda: queue[eng].dma_start(out, in_), reads, writes, sem=s, inc=16, extra=lat)

    def quant(q, p, t, n, reads, writes):
        op("V", 0.012 + 0.00022 * 4 * n * 1.25, lambda: g.vector.quantize_mx(q, p, t), reads, writes)

    tt, ts, tc = g.vector.tensor_tensor, g.vector.tensor_scalar, g.vector.tensor_copy
    scan, act = g.vector.tensor_tensor_scan, g.scalar.activation
    B4 = range(4)

    def copy(e, o, i, n, reads, writes, scale=1.0):
        if e == "A":
            A(n, lambda: act(o, i, ACTF.Copy, scale=scale), reads, writes)
        elif scale == 1.0:
            V(n, lambda: tc(o, i), reads, writes)
        else:
            V(n, lambda: ts(o, i, scale, None, ALU.mult), reads, writes)

    dma("S", T.xin[:], T.x[:], [], ["xin"])
    dma("AD", T.uin[:], T.u[:], [], ["uin"])
    dma("S", T.wq[:].bitcast(dt.uint8), T.wc[:], [], ["wq"])
    dma("AD", T.wp[:], T.ws[:], [], ["wp"])
    dma("S", T.vin[:], T.v[:], [], ["vin"])

    op("G", 0.2, lambda: g.iota(T.iw[:, 0:4], [[0, 4]], 0, 1), [], ["iw0"])
    V(258, lambda: g.vector.memset(T.full[:], 0.5), [], ["full"])
    op("G", 1.05, lambda: g.affine_select(T.eh[:], T.full[:], [[-1, 516]], ALU.is_equal, 0.0, 3, 4), ["full"], ["eh"])
    op("G", 0.6, lambda: g.iota(T.iob[:], [[1, 256]], 0, 0, allow_small_or_imprecise_dtypes=True), [], ["iob"])
    A(516, lambda: act(T.ef[:], T.eh[:], ACTF.Copy, scale=64.0), ["eh"], ["ef"])
    for e in ("eh", "ef"):
        for b in B4:
            quant(T[e + "q"][:, 128 * b:128 * b + 128], T[e + "p"][:, 128 * b:128 * b + 128], T[e][:, 3 - b:515 - b], 128, [e], ["%sq%d" % (e, b)])

    def col(k):
        return T.ib[:, k:k + 1]

    def fcol(k):
        return T.fb[:, k:k + 1]

    def bit(k, src, name, s1, o1, s2=None, o2=None):
        if o2 is None:
            V(1, lambda: ts(col(k), src, s1, None, o1), [name], ["ib%d" % k])
        else:
            V(1, lambda: ts(col(k), src, s1, s2, o1, o2), [name], ["ib%d" % k])
    p = T.iw[:, 0:1]
    bit(0, p, "iw0", 14, ALU.bitwise_and)
    bit(1, p, "iw0", 1, ALU.bitwise_and)
    bit(2, p, "iw0", 4, ALU.logical_shift_right, 1, ALU.bitwise_and)
    bit(3, p, "iw0", 7, ALU.bitwise_and, 1, ALU.logical_shift_right)
    bit(4, p, "iw0", 5, ALU.logical_shift_right)
    bit(5, p, "iw0", 4, ALU.logical_shift_right)
    V(1, lambda: tt(col(6), col(1), col(2), ALU.not_equal), ["ib1", "ib2"], ["ib6"])
    V(1, lambda: tt(col(7), col(0), col(2), ALU.add), ["ib0", "ib2"], ["ib7"])
    V(1, lambda: ts(fcol(0), col(7), -15.0, 497.0, ALU.mult, ALU.add), ["ib7"], ["fb0"])
    V(1, lambda: ts(fcol(1), col(7), 16.0, 15.0, ALU.mult, ALU.add), ["ib7"], ["fb1"])
    V(1, lambda: ts(T.seld[:, 0:1], col(6), fcol(0), fcol(1), ALU.mult, ALU.add), ["ib6", "fb0", "fb1"], ["seld"])
    V(1, lambda: ts(T.base[:], col(5), 16.0, 15.0, ALU.mult, ALU.add), ["ib5"], ["base"])
    V(1, lambda: tt(col(8), col(3), col(4), ALU.subtract), ["ib3", "ib4"], ["ib8"])
    bit(9, col(8), "ib8", 1, ALU.bitwise_and)
    bit(10, col(8), "ib8", 2, ALU.bitwise_and)
    V(1, lambda: tc(fcol(2), col(5)), ["ib5"], ["fb2"])
    V(1, lambda: ts(fcol(3), col(9), 16.0, fcol(2), ALU.mult, ALU.add), ["ib9", "fb2"], ["fb3"])
    V(1, lambda: ts(fcol(4), col(10), 4.0, fcol(3), ALU.mult, ALU.add), ["ib10", "fb3"], ["fb4"])
    V(1, lambda: ts(T.seln[:, 0:1], col(6), 32.0, fcol(4), ALU.mult, ALU.add), ["ib6", "fb4"], ["seln"])
    V(1, lambda: ts(fcol(5), col(5), float(NK), 128.0, ALU.is_ge, ALU.mult), ["ib5"], ["fb5"])
    V(1, lambda: ts(fcol(6), fcol(5), -255.5 / 128, 256.0, ALU.mult, ALU.add), ["fb5"], ["fb6"])
    A(256, lambda: act(T.top[:], T.iob[:], ACTF.Identity, bias=BIG, scale=0.0), ["iob"], ["top"])
    A(256, lambda: act(T.seg[:], T.iob[:], ACTF.Identity, bias=BIG, scale=0.0), ["iob"], ["seg0"])
    A(16, lambda: act(T.seg[:, 0:256:16], T.iob[:, 0:16], ACTF.Identity, bias=-BIG, scale=0.0), ["iob", "seg0"], ["seg0"])
    A(256, lambda: act(T.ones[:], T.iob[:], ACTF.Identity, bias=1.0, scale=0.0), ["iob"], ["ones"])
    A(256, lambda: act(T.cd[:, 256:512], T.iob[:], ACTF.Copy), ["iob"], ["cd0"])
    V(128, lambda: ts(T.k0[:], T.iob[:], 1.0 / 256, 4.0, ALU.mult, ALU.add), ["iob"], ["k0"])
    V(8, lambda: ts(T.kb[:, 0:8 * 264:264], T.iob[:, 0:8], 0.0, 16.0, ALU.mult, ALU.add), ["iob"], ["kbi"])
    V(8, lambda: g.vector.memset(T.rb[:, 0:8 * 264:264], -BIG), [], ["rbi"])
    V(1, lambda: g.vector.memset(T.rd[:, 0:1], 0.0), [], ["rd0"])

    def W(name, b):
        return (T[name + "q"][:, 128 * b:128 * b + 128], T[name + "p"][:, 128 * b:128 * b + 128])

    RUNS = [(c, 256 // H, "ab"[c * H // 256]) for c in range(0, 256, 256 // H)]
    quant(T.q0[:], T.p0[:], T.xin[:], 256, ["xin"], ["q0" + x for _, _, x in RUNS])
    quant(T.u0[:], T.s0[:], T.uin[:], 128, ["uin"], ["u0"])

    def halves(q, p):
        for b in B4:
            mm(("pr", b), W("eh", b), (T[q][:], T[p][:]), 256, True, True, ["ehq%d" % b] + [q + x for _, _, x in RUNS])
            if ZS[b] == "V":
                i, bn = bank(("pr", b))
                copy(TS[b], T.tp[:, 256 * b:256 * b + 256], i, 256, [], ["tp%d" % b, bn])

    early = [("pr", b) for b in B4 if ZS[b] == "V"] + [("pd", 2), ("pd", 3)]
    late = early[4:] + [("pr", b) for b in B4 if ZS[b] != "V"]
    SUMS = [[("pr", b) for b in B4]] if H == 1 else [early[:4], (late + early)[:4]]

    halves("q0", "p0")
    for r, h in enumerate(STEP):
        qn, pn, un, q2, p2, u2, s2 = "q%d" % r, "p%d" % r, "u%d" % r, "q%d" % (r + 1), "p%d" % (r + 1), "u%d" % (r + 1), "s%d" % (r + 1)
        Q, U, QN = (T[qn][:], T[pn][:]), (T[un][:], T["s%d" % r][:]), [qn + x for _, _, x in RUNS]
        dst = T.cores[(rank + h) % len(T.cores)]
        rid, pid, _ = topo.addr(dst)
        m, ne = topo.mask(core, dst), len(topo.engines(core, dst))

        def send(cost, lat, moves, reads, writes, arr, sent, rid=rid, pid=pid, m=m, ne=ne):
            def go():
                for o, i in moves:
                    g.remote_dma(o, i, T.sem[arr], T.sem[sent], pid, rid, m)
            op("G", cost, go, reads, [sent], sem=sent, inc=len(moves) * ne)
            op("N", lat, None, [sent], writes, sem=arr, inc=len(moves) * ne)

        mm(("pd", 0), U, Q, 256, True, True, QN + [un])
        for b in B4:
            at = ("pd", 2 + b % 2)
            mm(at, W("eh", b), U, 128, True, True, ["ehq%d" % b, un])
            i, bn = bank(at, 128)
            copy("A", T.du[:, 128 * b:128 * b + 128], i, 128, [], ["du%d" % b, bn])
        mm(("pd", 1), U, Q, 256, True, True, QN + [un])
        V(256, lambda: g.vector.transpose(T.st[:], T.pd[:, 0:256]), ["PD0"], ["st"])
        V(256, lambda: scan(T.rd[:, 1:257], T.seg[:], T.st[:], 0.0, ALU.min, ALU.max), ["seg0", "st"], ["rd"])
        V(256, lambda: tt(T.qd[:], T.rd[:, 0:256], T.st[:], ALU.is_ge), ["rd", "rd0", "st"], ["qd"], 2.0)
        V(256, lambda: scan(T.cd[:, 0:256], T.qd[:], T.qd[:], 0.0, ALU.mult, ALU.subtract), ["qd"], ["cd"], 0.5)
        for k in (0, 1):
            V(32, lambda k=k: g.vector.transpose(T.kt[:, 32 * k:32 * k + 32], T.cd[:, 15:512:16]), ["cd", "cd0"], ["kt%d" % k])
        V(32, lambda: g.vector.transpose(T.cd[:, 512:544], T.kt[:, 16:48]), ["kt0", "kt1"], ["ko"])
        GA(16, lambda: ts(T.offd[:], T.cd[:, 0:544].indirect(T.seld[:, 0:1]), -15.0, T.base[:], ALU.max, ALU.add), ["cd", "cd0", "ko", "seld", "base"], ["offd"])
        for (c, n, x), sums in zip(RUNS, SUMS):
            for b in B4:
                o, i = T.zt[:, 4 * c + b:4 * (c + n):4], T.du[:, 128 * b:128 * b + 128].indirect(T.offd[:, c // 16:(c + n) // 16])
                at = slice(256 * b + c, 256 * b + c + n)
                if ZS[b] == "V":
                    GA(n, lambda o=o, i=i, at=at: tt(o, i, T.tp[:, at], ALU.add), ["du%d" % b, "offd", "tp%d" % b], ["zt%d" % b + x])
                else:
                    AG(n, lambda i=i, at=at: act(T.ag[:, at], i, ACTF.Copy), ["du%d" % b, "offd"], ["ag%d" % b + x])
                    t, bn = bank(("pr", b), n, c)
                    V(n, lambda o=o, at=at, t=t: tt(o, T.ag[:, at], t, ALU.add), ["ag%d" % b + x, bn], ["zt%d" % b + x])
            Z = (T["zq%d" % r][:, c:c + n], T["zp%d" % r][:, c:c + n])
            quant(Z[0], Z[1], T.zt[:, 4 * c:4 * (c + n)], n, ["zt%d" % b + x for b in B4], ["zq%d" % r + x])
            for b in B4:
                mm(sums[b], W("ef", b), (T[qn][:, c:c + n], T[pn][:, c:c + n]), n, True, False, ["efq%d" % b, qn + x])
                mm(sums[b], W("w", b), Z, n, False, True, ["wq", "wp", "zq%d" % r + x])
                i, bn = bank(sums[b], n)
                copy(XS[b], T.xt[:, 4 * c + b:4 * (c + n):4], i, n, [], ["xt%d" % b + x, bn], 0.03125)
            quant(T[q2][:, c:c + n], T[p2][:, c:c + n], T.xt[:, 4 * c:4 * (c + n)], n, ["xt%d" % b + x for b in B4], [q2 + x])
            send(1.0, 1.0 + 2.0 / H, [(T["xl%d" % r][:, c:c + n].bitcast(dt.uint8), T[q2][:, c:c + n].bitcast(dt.uint8)),
                                      (T["xs%d" % r][:, c:c + n], T[p2][:, c:c + n])],
                 [q2 + x], ["xl%d" % r + x], "arr%s%d" % (x, r), "sent%s%d" % (x, r))
        if r < 2:
            halves(q2, p2)
        else:
            mm(("pd", 2), (T.vcq[:], T.vcp[:]), (T.q3[:], T.p3[:]), 256, True, True, ["vcq"] + ["q3" + x for _, _, x in RUNS])
            copy("A", T.ysb[:], bank(("pd", 2))[0], 256, [], ["ysb", "PD2"])
        for k in range(8):
            o, kk = 264 * k, slice(k, k + 1)
            run, v = T.rb[:, o + 1:o + 257], T.rb[:, o + 256:o + 257]
            cap, names = (T.top[:], ["top"]) if k == 0 else (T.rb[:, o - 264:o - 8], ["rb%d" % (k - 1), "rbi"])
            V(256, lambda run=run, cap=cap: scan(run, T.pd[:, 0:256], cap, -2.0 * BIG, ALU.max, ALU.min), names + ["PD0"], ["rb%d" % k])
            f, e, cn = [T[x][:, 256 * k:256 * k + 256] for x in ("sg", "ne", "cn")]
            if k % 2 and k < NK or k >= NK and NE[k] == "A":
                A(256, lambda f=f, v=v: act(f, T.pd[:, 512:768], ACTF.Sign, bias=v, scale=-1.0), ["rb%d" % k, "PD1"], ["sg%d" % k])
            if k % 2 and k < NK:
                j = k // 2
                V(128, lambda j=j, f=f: scan(T["k%d" % (j + 1)][:], f, T["k%d" % j][:], 1.0, ALU.min, ALU.add), ["sg%d" % k, "k%d" % j], ["k%d" % (j + 1)])
            if k < NK:
                continue
            if NE[k] == "A":
                A(256, lambda f=f, e=e: act(e, f, ACTF.Abs), ["sg%d" % k], ["ne%d" % k])
            else:
                V(256, lambda e=e, v=v: ts(e, T.pd[:, 0:256], v, None, ALU.not_equal), ["rb%d" % k, "PD0"], ["ne%d" % k])
            A(8, lambda k=k, v=v, kk=kk: act(T.junk[:, 8 * k:9 * k], T.rb[:, 256:264 * k:264], ACTF.Sign, bias=v, scale=-1.0, accum_out=T.ac[:, kk]),
              ["rb%d" % j for j in range(k + 1)], ["ac%d" % k], 0.08)
            V(128, lambda k=k, e=e, cn=cn: scan(cn, e, T.ones[:], k + 0.5, ALU.add, ALU.subtract), ["ne%d" % k, "ones"], ["cn%d" % k])
            A(256, lambda cn=cn, kk=kk: act(cn, cn, ACTF.Sign, bias=T.ac[:, kk], accum_out=T.nb[:, kk]), ["ac%d" % k], ["cn%d" % k, "nb%d" % k], 0.08)
        kn = "k%d" % (NK // 2)
        for k in range(NK):
            o = 264 * k
            if k == 0:
                V(128, lambda: scan(T.kb[:, 1:257], T[kn][:], T[kn][:], 16.0, ALU.min, ALU.min), [kn], ["kb0"])
            else:
                V(128, lambda o=o: scan(T.kb[:, o + 1:o + 257], T[kn][:], T.kb[:, o - 264:o - 8], 16.0, ALU.min, ALU.max), [kn, "kbi", "kb%d" % (k - 1)], ["kb%d" % k])
        KB = ["kb%d" % k for k in range(NK)]
        V(8, lambda: ts(T.fl[:, 0:NK], T.kb[:, 256:NK * 264:264], -0.498, None, ALU.add), KB, ["fl"])
        V(8, lambda: tt(T.nb[:, 0:NK], T.kb[:, 256:NK * 264:264], T.fl[:, 0:NK], ALU.subtract), KB + ["fl"], ["nbk"])
        NB = ["nbk"] + ["nb%d" % k for k in range(NK, 8)]
        copy("V", T.nb[0:64, 8:16], T.nb[64:128, 0:8], 8, NB, ["nh0"])
        copy("A", T.nb[64:128, 8:16], T.nb[0:64, 0:8], 8, NB, ["nh1"])
        NB = NB + ["nh0", "nh1"]
        for q in B4:
            copy(QS[q], T.nb[32 * q:32 * q + 32, 16:32], T.nb[32 * ((q + 1) % 4):32 * ((q + 1) % 4) + 32, 0:16], 16, NB, ["nx%d" % q])
        NX = NB + ["nx%d" % q for q in B4]
        for k in (0, 1):
            V(32, lambda k=k: g.vector.transpose(T.nt[:, 32 * k:32 * k + 32], T.nb[:, 0:32]), NX, ["nt%d" % k])
        V(32, lambda: g.vector.transpose(T.nb[:, 32:64], T.nt[:, 16:48]), ["nt0", "nt1"], ["no"])
        GA(16, lambda: ts(T.offn[:], T.nb[:, 0:64].indirect(T.seln[:, 0:1]), fcol(6), fcol(5), ALU.mult, ALU.add), NX + ["no", "seln", "fb5", "fb6"], ["offn"])
        send(0.5, 1.5, [(T["lo%d" % r][:], T.offn[:, 0:8])], ["offn"], ["lo%d" % r], "lst%d" % r, "lsent%d" % r)
        free = early if r < 2 else [("pr", b) for b in B4]
        for c, n, x in RUNS:
            for b in B4:
                at = free[b % len(free)]
                mm(at, W("ef", b), (T["xl%d" % r][:, c:c + n], T["xs%d" % r][:, c:c + n]), n, True, True, ["efq%d" % b, "xl%d" % r + x])
                i, bn = bank(at, n)
                copy(RS[b], T.tr[:, 256 * b + c:256 * b + c + n], i, n, [], ["tr%d" % b + x, bn], 0.03125)
        for b in B4:
            o, i = T.vt[:, b:512:4], T.tr[:, 256 * b:256 * b + 256].indirect(T["lo%d" % r][:, 0:8])
            need = ["tr%d" % b + x for _, _, x in RUNS] + ["lo%d" % r]
            if VS[b] == "A":
                AG(128, lambda o=o, i=i: act(o, i, ACTF.Copy), need, ["vt%d" % b])
            else:
                GA(128, lambda o=o, i=i: tc(o, i), need, ["vt%d" % b])
        quant(T[u2][:], T[s2][:], T.vt[:], 128, ["vt%d" % b for b in B4], [u2])
        if r == 0:
            quant(T.vcq[:], T.vcp[:], T.vin[:], 128, ["vin"], ["vcq"])
    Q3 = ["q3" + x for _, _, x in RUNS]
    dma("S", T.oc[:], T.q3[:].bitcast(dt.uint8), Q3, [])
    for k in B4:
        dma("S", T.osc[4 * k:4 * k + 4, :], T.p3[32 * k:32 * k + 4, :], Q3, [])
    dma("S", T.y[:], T.ysb[:], ["ysb"], [])
    AG(256, lambda: act(T.opk[:], T.iob[:].indirect(T.offd[:, 0:16]), ACTF.Copy), ["iob", "offd"], ["opk"])
    AG(128, lambda: act(T.opn[:], T.iob[:].indirect(T.offn[:, 0:8]), ACTF.Copy), ["iob", "offn"], ["opn"])
    dma("S", T["op"][:, 0:256], T.opk[0:128:16, :], ["opk"], [])
    dma("S", T["op"][:, 256:384], T.opn[0:128:16, :], ["opn"], [])
    dma("S", T.uc[:], T.u3[:].bitcast(dt.uint8), ["u3"], [])
    for k in B4:
        dma("AD" if k % 2 else "S", T.usc[4 * k:4 * k + 4, :], T.s3[32 * k:32 * k + 4, :], ["u3"], [])
    plan_and_emit(g, T, ops, queue, csem)


TRIES, MOVES, FOUND = 600, 60000, {}
ASSUMED = [(0.8, 0.2, 0.0), (1.0, 0.07, 0.5), (1.2, 0.25, -0.5)]


def find_order(ops):
    n = len(ops)
    unit, cost, extra, hard = [o["u"] for o in ops], [o["cost"] for o in ops], [o["extra"] for o in ops], [sorted(o["hard"]) for o in ops]
    pred = [sorted(o["hard"] | o["order"]) for o in ops]
    succ = [[] for _ in range(n)]
    for k in range(n):
        for d in pred[k]:
            succ[d].append(k)
    takes = [[late + cost[k] if unit[k] == "N" else cost[k] * f if unit[k] in "VAP" else cost[k] for k in range(n)] for f, _, late in ASSUMED]
    wake0, take0 = ASSUMED[0][1], takes[0]
    tail = [0.0] * n
    for k in range(n - 1, -1, -1):
        tail[k] = take0[k] + extra[k] + max([tail[s] + wake0 for s in succ[k]] + [0.0])

    def plan(key):
        left, free, end, seq = [len(d) for d in pred], {u: 0.0 for u in unit}, [0.0] * n, []
        ready = {k: 0.0 for k in range(n) if left[k] == 0}
        while ready:
            est = [(max(t, free[unit[k]]), k) for k, t in ready.items()]
            lo = min(est)[0] + 0.06
            t, k = max((e for e in est if e[0] <= lo), key=lambda e: (key[e[1]], -e[1]))
            free[unit[k]] = 0.0 if unit[k] == "N" else t + take0[k]
            end[k] = t + take0[k] + extra[k]
            seq.append(k)
            del ready[k]
            for s in succ[k]:
                left[s] -= 1
                if left[s] == 0:
                    ready[s] = max([end[d] + wake0 for d in hard[s]] + [0.0])
        return seq

    def ends(seq):
        total = 0.0
        for (_, wake, _), take in zip(ASSUMED, takes):
            free, end = {u: 0.0 for u in "VAPGSN"}, [0.0] * n
            for k in seq:
                u = unit[k]
                t = free[u]
                for d in hard[k]:
                    if end[d] > t:
                        t = end[d]
                t += take[k]
                if u != "N":
                    free[u] = t
                end[k] = t + extra[k] + wake
            total += max(end) + 0.0005 * sum(end) / n
        return total

    state = [12345]

    def rnd(m):
        state[0] = (state[0] * 1103515245 + 12345) % 2147483648
        return (state[0] >> 8) % m
    key = tail
    best = plan(key)
    least = ends(best)
    for i in range(TRIES):
        trial = list(key)
        for _ in range(n if i < 40 else (2, 5, 12)[rnd(3)]):
            trial[_ if i < 40 else rnd(n)] += (rnd(1000) / 1000.0) * 0.4 if i < 40 else (rnd(1000) + rnd(1000) - 1000) / 700.0
        seq = plan(trial)
        e = ends(seq)
        if e < least:
            best, least, key = seq, e, trial
    seq, now = list(best), least
    for i in range(MOVES):
        a = rnd(n)
        k = seq[a]
        step, b, left = (1, -1)[rnd(2)], a, 1 + (0, 0, 1, 2)[rnd(4)]
        stop = succ[k] if step == 1 else pred[k]
        while left and 0 <= b + step < n and seq[b + step] not in stop:
            b += step
            left -= unit[seq[b]] == unit[k]
        if left:
            continue
        trial = seq[:a] + seq[a + 1:]
        trial.insert(b, k)
        e = ends(trial)
        if e < now + 0.25 * (1.0 - i / MOVES) ** 2 * rnd(1000) / 1000.0:
            seq, now = trial, e
            if e < least:
                best, least = trial, e
    return best


def plan_and_emit(g, T, ops, queue, csem):
    if len(ops) not in FOUND:
        FOUND[len(ops)] = find_order(ops)
    count, clock, after = {}, {}, {}
    for i, k in enumerate(FOUND[len(ops)]):
        o = ops[k]
        known = clock.setdefault(o["u"], {})
        need = {}
        for d in sorted(o["hard"], key=lambda d: -after[d][2]):
            s, v, _, seen = after[d]
            if known.get(s, 0) >= v:
                continue
            need[s] = max(need.get(s, 0), v)
            for a, b in seen.items():
                known[a] = max(known.get(a, 0), b)
            known[s] = max(known.get(s, 0), v)
        if o["fn"] is not None:
            for s, v in need.items():
                queue[o["eng"]].wait_ge(T.sem[s], v)
        s = o["sem"] or csem[o["eng"]]
        count[s] = count.get(s, 0) + o["inc"]
        if o["fn"] is not None:
            c = o["fn"]()
            if c is not None:
                c.then_inc(T.sem[s], o["inc"])
        after[k] = (s, count[s], i, dict(known) if o["fn"] is not None else {})
    for s, v in count.items():
        if clock["G"].get(s, 0) < v:
            g.wait_ge(T.sem[s], v)
